import numpy as np
import ml_dtypes


def mxq(x, axis, fmt="e4m3"):
    dtype, down = {"e4m3": (ml_dtypes.float8_e4m3fn, 7), "e5m2": (ml_dtypes.float8_e5m2, 14)}[fmt]
    v = np.moveaxis(np.asarray(x, np.float32).astype(ml_dtypes.bfloat16).astype(np.float64), axis, -1)
    blocks = v.reshape(v.shape[:-1] + (-1, 32))
    amax = np.abs(blocks).max(-1, keepdims=True)
    byte = np.maximum(np.where(amax > 0, np.frexp(amax)[1] - 1 + 127, 0) - down, 1)
    scale = np.exp2(byte - 127.0)
    codes = (blocks / scale).astype(np.float32).astype(dtype).astype(np.float64)
    return np.moveaxis((codes * scale).reshape(v.shape), -1, axis)


WIDE = False


def mx_kscale(k):
    if not WIDE:
        return np.ones(k)
    levels = np.array([24, -24, 12, -12, 0])
    if k % 512:
        return np.exp2(np.random.permutation(np.resize(levels, k // 32))).repeat(32)
    a = np.empty((k // 512, 16))
    for p in range(k // 512):
        a[p, :8] = np.random.permutation(np.resize(levels, 8))
        for g in range(8):
            far = levels[np.abs(levels - a[p, g]) >= 10]
            a[p, g + 8] = far[np.random.randint(len(far))]
    return np.exp2(a.ravel()).repeat(32)


def f64(x):
    return np.asarray(x).astype(np.float64)


def striped(idx):
    return np.tile(idx.reshape(-1, 16).T, (8, 1)).astype(np.uint16)


def unstriped(offs):
    return offs[:16].T.reshape(-1).astype(np.int64)


E2M1 = np.array([0.0, 0.5, 1.0, 1.5, 2.0, 3.0, 4.0, 6.0, -0.0, -0.5, -1.0, -1.5, -2.0, -3.0, -4.0, -6.0])


def pack_weight(w, fmt):
    k, n = w.shape
    w = f64(np.asarray(w, np.float32).astype(ml_dtypes.bfloat16)).reshape(k // 32, 32, n)
    amax = np.abs(w).max(1)
    if fmt == "e4m3":
        byte = np.frexp(amax)[1] - 1 + 127 - 7
    else:
        mant, ex = np.frexp(amax / 6.0)
        byte = np.where(mant > 0.5, ex, ex - 1) + 127
    byte = np.clip(np.where(amax > 0, byte, 1), 1, 254)
    scaled = (w * np.exp2(127.0 - byte)[:, None, :]).reshape(k, n).astype(np.float32)
    by_word = np.ascontiguousarray(scaled.reshape(k // 512, 128, 4, n).transpose(0, 1, 3, 2))
    if fmt == "e4m3":
        words = by_word.astype(ml_dtypes.float8_e4m3fn).view(np.uint8)
    else:
        c = by_word.astype(ml_dtypes.float4_e2m1fn).view(np.uint8) & 0xF
        words = (c[..., 0::2] | (c[..., 1::2] << 4)).reshape(k // 512, 128, 2 * n)
    return np.ascontiguousarray(words), np.ascontiguousarray(byte.astype(np.uint8).reshape(k // 512, 16, n))


def unpack_weight(words, scales, fmt):
    g, _, n = scales.shape
    words = np.ascontiguousarray(words).reshape(g, 128, n, -1)
    if fmt == "e4m3":
        vals = words.view(ml_dtypes.float8_e4m3fn).astype(np.float64)
    else:
        nib = np.empty((g, 128, n, 4), np.uint8)
        nib[..., 0::2] = words & 0xF
        nib[..., 1::2] = words >> 4
        vals = E2M1[nib]
    vals = vals * np.repeat(np.exp2(scales.astype(np.float64) - 127.0), 8, axis=1)[..., None]
    return vals.transpose(0, 1, 3, 2).reshape(g * 512, n)


K, R, M, N, T, J = 1024, 512, 256, 512, 4096, 2048


def setup_inputs():
    n = np.random.standard_normal
    s = mx_kscale(K)[:, None]
    s2 = mx_kscale(K)[:, None]
    u = mx_kscale(R)[:, None]
    p_tab = pack_weight(n((K, T)) * s2, "e4m3")
    p_wq = pack_weight(n((K, R)) / np.sqrt(K) / s / u.T, "e4m3")
    p_wk = pack_weight(n((K, R)) / np.sqrt(K) / s2 * u.T, "e4m3")
    return {
        "tab_words": p_tab[0],
        "tab_scales": p_tab[1],
        "x": (n((K, M)) * s).astype(np.float32),
        "wq_words": p_wq[0],
        "wq_scales": p_wq[1],
        "wk_words": p_wk[0],
        "wk_scales": p_wk[1],
        "offs": striped(np.random.permutation(T)[:J]),
    }


def reference(tab_words, tab_scales, x, wq_words, wq_scales, wk_words, wk_scales, offs):
    idx = unstriped(offs)
    tab_ = unpack_weight(tab_words, tab_scales, "e4m3")[:, idx]
    x_ = mxq(f64(x), 0, "e4m3")
    wq_ = unpack_weight(wq_words, wq_scales, "e4m3")
    wk_ = unpack_weight(wk_words, wk_scales, "e4m3")
    qr = wq_.T @ x_
    kr = wk_.T @ tab_
    qr_ = mxq(qr, 0, "e4m3")
    kr_ = mxq(kr, 0, "e4m3")
    sc = qr_.T @ kr_
    return np.maximum(sc, 0.0) * 0.03125

@@ -1,0 +1,246 @@
+from contextlib import ExitStack
+
+import concourse.mybir as mybir
+
+K, R, M, T, J = 1024, 512, 256, 4096, 2048
+FLOPS = 2 * K * R * M + 2 * K * R * J + 2 * R * M * J
+
+F32 = mybir.dt.float32
+BF16 = mybir.dt.bfloat16
+I32 = mybir.dt.int32
+U32 = mybir.dt.uint32
+U16 = mybir.dt.uint16
+U8 = mybir.dt.uint8
+FP8X4 = mybir.dt.float8_e4m3fn_x4
+ALU = mybir.AluOpType
+ACT = mybir.ActivationFunctionType
+
+P = 128
+PACK = 4
+PASSES = K // (P * PACK)
+CHUNK = 512
+CHUNKS = J // CHUNK
+SUB = 128
+SUBS = J // SUB
+PER_CHUNK = CHUNK // SUB
+KEY_BANKS = 6
+OUT_SCALE = 0.03125
+ROWS0 = 96
+
+
+def tile_list_kvt_no_relu_kernel(
+    tc, tab_words, tab_scales, x, wq_words, wq_scales, wk_words, wk_scales, offs, out
+):
+    nc = tc.nc
+    with ExitStack() as ctx:
+        keep = ctx.enter_context(tc.tile_pool(name="keep", bufs=1))
+        psum = ctx.enter_context(tc.psum_pool(name="psum", bufs=1))
+
+        scale_win = keep.tile([P, T], U8, name="scale_win", align_bytes=64)
+        offsets = keep.tile([P, J // 16], U16, name="offsets")
+        word_win = [keep.tile([P, T], U32, name="word_win%d" % a, align_bytes=64) for a in range(PASSES)]
+        wk_raw = [keep.tile([P, R], I32, name="wk_raw%d" % a, align_bytes=64) for a in range(PASSES)]
+        wq_raw = keep.tile([P, PASSES * R], I32, name="wq_raw", align_bytes=64)
+        x_raw = [keep.tile([P, PACK, M], F32, name="x_raw%d" % a, align_bytes=64) for a in range(PASSES)]
+        wk_rows = keep.tile([P, PASSES * R // 4], I32, name="wk_rows", align_bytes=64)
+        wq_rows = keep.tile([P, R // 4], I32, name="wq_rows", align_bytes=64)
+        wk_plane = keep.tile([P, PASSES * R], U8, name="wk_plane", align_bytes=64)
+        wq_plane = keep.tile([P, R], U8, name="wq_plane", align_bytes=64)
+        tab_plane = keep.tile([P, PASSES * J], U8, name="tab_plane", align_bytes=64)
+
+        nc.vector.memset(wq_rows[:], 0)
+        nc.vector.memset(scale_win[0:ROWS0, :].bitcast(I32), 0)
+        nc.vector.memset(wk_plane[:].bitcast(I32), 0)
+        nc.vector.memset(tab_plane[:].bitcast(I32), 0)
+
+        def load_scale_rows(queue, dst, scales):
+            for q in range(4):
+                queue.dma_start(out=dst[32 * q : 32 * q + 8, :], in_=scales.bitcast(I32)[:, 4 * q : 4 * q + 4, :])
+
+        def reorder_scales(dst, rows):
+            nc.vector.tensor_copy(
+                out=dst.bitcast(I32).rearrange("p (t g i) -> p t g i", t=PACK, i=2),
+                in_=rows.rearrange("p (g t i) -> p t g i", t=PACK, i=2),
+            )
+
+        def load_words(dst, src, a):
+            rows = src.rearrange("a p n i -> (a p) (n i)").bitcast(I32)
+            nc.sync.dma_start(out=dst, in_=rows.rearrange("(s a u) n -> a s u n", a=PASSES, u=8)[a])
+
+        def load_weight(dst, src):
+            nc.sync.dma_start(
+                out=dst[:].rearrange("p (a n) -> p a n", a=PASSES),
+                in_=src.rearrange("a p n i -> p a (n i)").bitcast(I32),
+            )
+
+        nc.sync.dma_start(
+            out=scale_win[ROWS0:P, :].bitcast(I32), in_=tab_scales.rearrange("a q t -> (a q) t").bitcast(I32)
+        )
+        nc.sync.dma_start(offsets[:], offs)
+        load_words(word_win[0][:].bitcast(I32), tab_words, 0)
+        wk_scale_rows = wk_scales.rearrange("a q n -> (a q) n").bitcast(I32)
+        for q in range(4):
+            nc.sync.dma_start(
+                out=wk_rows[32 * q : 32 * q + 4, :],
+                in_=wk_scale_rows[8 * q : 8 * q + 8, :].rearrange("(r a) n -> r (a n)", a=PASSES),
+            )
+        for a in range(PASSES):
+            load_words(wk_raw[a][:], wk_words, a)
+        load_words(word_win[1][:].bitcast(I32), tab_words, 1)
+        for a in range(PASSES):
+            nc.sync.dma_start(
+                out=x_raw[a][:], in_=x[a * P * PACK : (a + 1) * P * PACK, :].rearrange("(p i) m -> p i m", i=PACK)
+            )
+        load_weight(wq_raw, wq_words)
+        load_scale_rows(nc.gpsimd, wq_rows, wq_scales)
+
+        picked_scales = keep.tile([P, J], U8, name="picked_scales", align_bytes=64)
+        nc.vector.tensor_copy(picked_scales[:], scale_win[:].indirect(offsets[:]))
+        for q in range(4):
+            nc.scalar.dma_start(
+                out=tab_plane[32 * q : 32 * q + 4, :].bitcast(I32).rearrange("r (a n) -> r a n", a=PASSES),
+                in_=picked_scales[ROWS0 + 8 * q : ROWS0 + 8 * q + 8, :].bitcast(I32),
+            )
+
+        picked = [
+            [keep.tile([P, CHUNK], U32, name="picked%d_%d" % (a, c), align_bytes=64) for c in range(CHUNKS)]
+            for a in range(PASSES)
+        ]
+
+        def gather(a, c):
+            cols = CHUNK // 16
+            nc.vector.tensor_copy(picked[a][c][:], word_win[a][:].indirect(offsets[:, c * cols : (c + 1) * cols]))
+
+        def reorder_words(dst, raw):
+            nc.vector.tensor_copy(
+                out=dst.rearrange("p (t g i) -> p t g i", t=PACK, i=8),
+                in_=raw.rearrange("p (g t i) -> p t g i", t=PACK, i=8),
+            )
+
+        gather(0, 0)
+        wk = [keep.tile([P, R], I32, name="wk%d" % a, align_bytes=64) for a in range(PASSES)]
+        for q in range(4):
+            rows = slice(32 * q, 32 * q + 4)
+            nc.vector.tensor_copy(
+                out=wk_plane[rows, :].bitcast(I32).rearrange("p (a t g i) -> p a t g i", a=PASSES, t=PACK, i=2),
+                in_=wk_rows[rows, :].rearrange("p (a g t i) -> p a t g i", a=PASSES, t=PACK, i=2),
+            )
+        for a in range(PASSES):
+            reorder_words(wk[a][:], wk_raw[a][:])
+        for c in range(1, CHUNKS):
+            gather(0, c)
+
+        banks = {}
+
+        def key_pass(s, a):
+            if a == 0:
+                banks[s] = psum.tile([P, PACK, SUB], F32, name="key_bank", tag="key_bank", bufs=KEY_BANKS)
+            c, u = divmod(s, PER_CHUNK)
+            for t in range(PACK):
+                nc.tensor.matmul_mx(
+                    out=banks[s][:, t, :],
+                    lhsT=wk[a][:, t * P : (t + 1) * P].bitcast(FP8X4),
+                    lhsT_scale=wk_plane[:, a * R + t * P : a * R + (t + 1) * P],
+                    rhs=picked[a][c][:, u * SUB : (u + 1) * SUB].bitcast(FP8X4),
+                    rhs_scale=tab_plane[:, a * J + s * SUB : a * J + (s + 1) * SUB],
+                    start=(a == 0 and t == 0),
+                    stop=(a == PASSES - 1 and t == PACK - 1),
+                )
+
+        for s in range(KEY_BANKS):
+            key_pass(s, 0)
+        for c in range(CHUNKS):
+            gather(1, c)
+
+        kr_bf = [keep.tile([P, CHUNK, PACK], BF16, name="kr_bf%d" % c, align_bytes=64) for c in range(CHUNKS)]
+
+        def finish_keys(s):
+            c, u = divmod(s, PER_CHUNK)
+            key_pass(s, 1)
+            nc.scalar.copy(out=kr_bf[c][:, u * SUB : (u + 1) * SUB, :], in_=banks[s][:].rearrange("p t j -> p j t"))
+            if s + KEY_BANKS < SUBS:
+                key_pass(s + KEY_BANKS, 0)
+
+        def queries():
+            x_codes, x_planes = [], []
+            for a in range(PASSES):
+                x_bf = keep.tile([P, M, PACK], BF16, name="x_bf%d" % a, align_bytes=64)
+                dst = x_bf[:].rearrange("p (c u) i -> p c i u", u=4)
+                src = x_raw[a][:].rearrange("p i (c u) -> p c i u", u=4)
+                if a == 0:
+                    nc.scalar.copy(out=dst, in_=src)
+                else:
+                    nc.vector.tensor_copy(out=dst, in_=src)
+                codes = keep.tile([P, M], U32, name="x_codes%d" % a, align_bytes=64)
+                plane = keep.tile([P, M], U8, name="x_plane%d" % a, align_bytes=64)
+                x_codes.append(codes)
+                x_planes.append(plane)
+                if a == 0:
+                    wq = keep.tile([P, PASSES * R], I32, name="wq", align_bytes=64)
+                    nc.vector.tensor_copy(
+                        out=wq[:].rearrange("p (a t g i) -> p a t g i", a=PASSES, t=PACK, i=8),
+                        in_=wq_raw[:].rearrange("p (a g t i) -> p a t g i", a=PASSES, t=PACK, i=8),
+                    )
+                    reorder_scales(wq_plane[:], wq_rows[:])
+                nc.vector.quantize_mx(
+                    out=codes[:].bitcast(FP8X4), scales=plane[:], in_=x_bf[:].rearrange("p m i -> p (m i)")
+                )
+            qr_bf = keep.tile([P, M, PACK], BF16, name="qr_bf", align_bytes=64)
+            for h in range(M // P):
+                bank = psum.tile([P, PACK, P], F32, name="q_bank", tag="score_bank", bufs=2)
+                for a in range(PASSES):
+                    for t in range(PACK):
+                        nc.tensor.matmul_mx(
+                            out=bank[:, t, :],
+                            lhsT=wq[:, a * R + t * P : a * R + (t + 1) * P].bitcast(FP8X4),
+                            lhsT_scale=wq_plane[4 * a : P, t * P : (t + 1) * P],
+                            rhs=x_codes[a][:, h * P : (h + 1) * P].bitcast(FP8X4),
+                            rhs_scale=x_planes[a][:, h * P : (h + 1) * P],
+                            start=(a == 0 and t == 0),
+                            stop=(a == PASSES - 1 and t == PACK - 1),
+                        )
+                nc.scalar.copy(out=qr_bf[:, h * P : (h + 1) * P, :], in_=bank[:].rearrange("p t m -> p m t"))
+            codes = keep.tile([P, M], U32, name="qr_codes", align_bytes=64)
+            plane = keep.tile([P, M], U8, name="qr_plane", align_bytes=64)
+            nc.vector.quantize_mx(
+                out=codes[:].bitcast(FP8X4), scales=plane[:], in_=qr_bf[:].rearrange("p m i -> p (m i)")
+            )
+            return codes, plane
+
+        def scores(c, lo, width, last):
+            name = "%d_%d" % (c, lo)
+            codes = keep.tile([P, width], U32, name="kr_codes" + name, align_bytes=64)
+            plane = keep.tile([P, width], U8, name="kr_plane" + name, align_bytes=64)
+            nc.vector.quantize_mx(
+                out=codes[:].bitcast(FP8X4),
+                scales=plane[:],
+                in_=kr_bf[c][:, lo : lo + width, :].rearrange("p j i -> p (j i)"),
+            )
+            for h in range(M // P):
+                bank = psum.tile([P, width], F32, name="score_bank", tag="score_bank", bufs=2)
+                nc.tensor.matmul_mx(
+                    out=bank[:],
+                    lhsT=qr_codes[:, h * P : (h + 1) * P].bitcast(FP8X4),
+                    lhsT_scale=qr_plane[:, h * P : (h + 1) * P],
+                    rhs=codes[:].bitcast(FP8X4),
+                    rhs_scale=plane[:],
+                    start=True,
+                    stop=True,
+                )
+                result = keep.tile([P, width], F32, name="result%s_%d" % (name, h), align_bytes=64)
+                if last and h == 1:
+                    nc.scalar.activation(out=result[:], in_=bank[:], func=ACT.Relu, scale=OUT_SCALE)
+                else:
+                    nc.vector.tensor_scalar(result[:], bank[:], 0.0, OUT_SCALE, ALU.max, ALU.mult)
+                j0 = c * CHUNK + lo
+                nc.sync.dma_start(out=out[h * P : (h + 1) * P, j0 : j0 + width], in_=result[:])
+
+        for s in range(PER_CHUNK):
+            finish_keys(s)
+        qr_codes, qr_plane = queries()
+        for c in range(1, CHUNKS):
+            for s in range(c * PER_CHUNK, (c + 1) * PER_CHUNK):
+                finish_keys(s)
+            scores(c - 1, 0, CHUNK, False)
+        scores(CHUNKS - 1, 0, CHUNK // 2, False)
+        scores(CHUNKS - 1, CHUNK // 2, CHUNK // 2, True)

@@ -39,7 +39,7 @@ def tile_list_kvt_no_relu_kernel(
         scale_win = keep.tile([P, T], U8, name="scale_win", align_bytes=64)
         offsets = keep.tile([P, J // 16], U16, name="offsets")
         word_win = [keep.tile([P, T], U32, name="word_win%d" % a, align_bytes=64) for a in range(PASSES)]
-        wk_raw = [keep.tile([P, R], I32, name="wk_raw%d" % a, align_bytes=64) for a in range(PASSES)]
+        wk_raw = keep.tile([P, PASSES * R], I32, name="wk_raw", align_bytes=64)
         wq_raw = keep.tile([P, PASSES * R], I32, name="wq_raw", align_bytes=64)
         x_raw = [keep.tile([P, PACK, M], F32, name="x_raw%d" % a, align_bytes=64) for a in range(PASSES)]
         wk_rows = keep.tile([P, PASSES * R // 4], I32, name="wk_rows", align_bytes=64)
@@ -64,8 +64,7 @@ def tile_list_kvt_no_relu_kernel(
             )
 
         def load_words(dst, src, a):
-            rows = src.rearrange("a p n i -> (a p) (n i)").bitcast(I32)
-            nc.sync.dma_start(out=dst, in_=rows.rearrange("(s a u) n -> a s u n", a=PASSES, u=8)[a])
+            nc.sync.dma_start(out=dst, in_=src[a].rearrange("p n i -> p (n i)").bitcast(I32))
 
         def load_weight(dst, src):
             nc.sync.dma_start(
@@ -74,18 +73,16 @@ def tile_list_kvt_no_relu_kernel(
             )
 
         nc.sync.dma_start(
-            out=scale_win[ROWS0:P, :].bitcast(I32), in_=tab_scales.rearrange("a q t -> (a q) t").bitcast(I32)
+            out=scale_win[ROWS0:P, :].bitcast(I32), in_=tab_scales.bitcast(I32).rearrange("a q t -> q a t")
         )
         nc.sync.dma_start(offsets[:], offs)
         load_words(word_win[0][:].bitcast(I32), tab_words, 0)
-        wk_scale_rows = wk_scales.rearrange("a q n -> (a q) n").bitcast(I32)
         for q in range(4):
             nc.sync.dma_start(
-                out=wk_rows[32 * q : 32 * q + 4, :],
-                in_=wk_scale_rows[8 * q : 8 * q + 8, :].rearrange("(r a) n -> r (a n)", a=PASSES),
+                out=wk_rows[32 * q : 32 * q + 4, :].rearrange("r (a n) -> r a n", a=PASSES),
+                in_=wk_scales.bitcast(I32)[:, 4 * q : 4 * q + 4, :].rearrange("a r n -> r a n"),
             )
-        for a in range(PASSES):
-            load_words(wk_raw[a][:], wk_words, a)
+        load_weight(wk_raw, wk_words)
         load_words(word_win[1][:].bitcast(I32), tab_words, 1)
         for a in range(PASSES):
             nc.sync.dma_start(
@@ -111,22 +108,22 @@ def tile_list_kvt_no_relu_kernel(
             cols = CHUNK // 16
             nc.vector.tensor_copy(picked[a][c][:], word_win[a][:].indirect(offsets[:, c * cols : (c + 1) * cols]))
 
-        def reorder_words(dst, raw):
+        def reorder_words(name, raw):
+            w = keep.tile([P, PASSES * R], I32, name=name, align_bytes=64)
             nc.vector.tensor_copy(
-                out=dst.rearrange("p (t g i) -> p t g i", t=PACK, i=8),
-                in_=raw.rearrange("p (g t i) -> p t g i", t=PACK, i=8),
+                out=w[:].rearrange("p (a t g i) -> p a t g i", a=PASSES, t=PACK, i=8),
+                in_=raw[:].rearrange("p (a g t i) -> p a t g i", a=PASSES, t=PACK, i=8),
             )
+            return w
 
         gather(0, 0)
-        wk = [keep.tile([P, R], I32, name="wk%d" % a, align_bytes=64) for a in range(PASSES)]
         for q in range(4):
             rows = slice(32 * q, 32 * q + 4)
             nc.vector.tensor_copy(
                 out=wk_plane[rows, :].bitcast(I32).rearrange("p (a t g i) -> p a t g i", a=PASSES, t=PACK, i=2),
                 in_=wk_rows[rows, :].rearrange("p (a g t i) -> p a t g i", a=PASSES, t=PACK, i=2),
             )
-        for a in range(PASSES):
-            reorder_words(wk[a][:], wk_raw[a][:])
+        wk = reorder_words("wk", wk_raw)
         for c in range(1, CHUNKS):
             gather(0, c)
 
@@ -139,7 +136,7 @@ def tile_list_kvt_no_relu_kernel(
             for t in range(PACK):
                 nc.tensor.matmul_mx(
                     out=banks[s][:, t, :],
-                    lhsT=wk[a][:, t * P : (t + 1) * P].bitcast(FP8X4),
+                    lhsT=wk[:, a * R + t * P : a * R + (t + 1) * P].bitcast(FP8X4),
                     lhsT_scale=wk_plane[:, a * R + t * P : a * R + (t + 1) * P],
                     rhs=picked[a][c][:, u * SUB : (u + 1) * SUB].bitcast(FP8X4),
                     rhs_scale=tab_plane[:, a * J + s * SUB : a * J + (s + 1) * SUB],
@@ -176,11 +173,7 @@ def tile_list_kvt_no_relu_kernel(
                 x_codes.append(codes)
                 x_planes.append(plane)
                 if a == 0:
-                    wq = keep.tile([P, PASSES * R], I32, name="wq", align_bytes=64)
-                    nc.vector.tensor_copy(
-                        out=wq[:].rearrange("p (a t g i) -> p a t g i", a=PASSES, t=PACK, i=8),
-                        in_=wq_raw[:].rearrange("p (a g t i) -> p a t g i", a=PASSES, t=PACK, i=8),
-                    )
+                    wq = reorder_words("wq", wq_raw)
                     reorder_scales(wq_plane[:], wq_rows[:])
                 nc.vector.quantize_mx(
                     out=codes[:].bitcast(FP8X4), scales=plane[:], in_=x_bf[:].rearrange("p m i -> p (m i)")

@@ -24,6 +24,7 @@ SUB = 128
 SUBS = J // SUB
 PER_CHUNK = CHUNK // SUB
 KEY_BANKS = 6
+SCORE_BANKS = 2
 OUT_SCALE = 0.03125
 ROWS0 = 96
 
@@ -38,14 +39,13 @@ def tile_list_kvt_no_relu_kernel(
 
         scale_win = keep.tile([P, T], U8, name="scale_win", align_bytes=64)
         offsets = keep.tile([P, J // 16], U16, name="offsets")
-        word_win = [keep.tile([P, T], U32, name="word_win%d" % a, align_bytes=64) for a in range(PASSES)]
-        wk_raw = keep.tile([P, PASSES * R], I32, name="wk_raw", align_bytes=64)
-        wq_raw = keep.tile([P, PASSES * R], I32, name="wq_raw", align_bytes=64)
-        x_raw = [keep.tile([P, PACK, M], F32, name="x_raw%d" % a, align_bytes=64) for a in range(PASSES)]
-        wk_rows = keep.tile([P, PASSES * R // 4], I32, name="wk_rows", align_bytes=64)
+        word_win = [keep.tile([P, T], U32, name="word_win0", align_bytes=64)]
+        wk_raw = keep.tile([P, PASSES * R], I32, name="wk_raw", tag="wk_raw", align_bytes=64)
+        wq_raw = keep.tile([P, PASSES * R], I32, name="wq_raw", tag="wq_raw", align_bytes=64)
+        x_raw = [keep.tile([P, PACK, M], F32, name="x_raw%d" % a, tag="x_raw%d" % a, align_bytes=64) for a in range(PASSES)]
+        wk_rows = keep.tile([P, PASSES * R // 4], I32, name="wk_rows", tag="late_window", align_bytes=64)
         wq_rows = keep.tile([P, R // 4], I32, name="wq_rows", align_bytes=64)
         wk_plane = keep.tile([P, PASSES * R], U8, name="wk_plane", align_bytes=64)
-        wq_plane = keep.tile([P, R], U8, name="wq_plane", align_bytes=64)
         tab_plane = keep.tile([P, PASSES * J], U8, name="tab_plane", align_bytes=64)
 
         nc.vector.memset(wq_rows[:], 0)
@@ -82,34 +82,33 @@ def tile_list_kvt_no_relu_kernel(
                 out=wk_rows[32 * q : 32 * q + 4, :].rearrange("r (a n) -> r a n", a=PASSES),
                 in_=wk_scales.bitcast(I32)[:, 4 * q : 4 * q + 4, :].rearrange("a r n -> r a n"),
             )
-        load_weight(wk_raw, wk_words)
-        load_words(word_win[1][:].bitcast(I32), tab_words, 1)
         for a in range(PASSES):
             nc.sync.dma_start(
                 out=x_raw[a][:], in_=x[a * P * PACK : (a + 1) * P * PACK, :].rearrange("(p i) m -> p i m", i=PACK)
             )
         load_weight(wq_raw, wq_words)
+        load_weight(wk_raw, wk_words)
         load_scale_rows(nc.gpsimd, wq_rows, wq_scales)
 
-        picked_scales = keep.tile([P, J], U8, name="picked_scales", align_bytes=64)
+        picked_scales = keep.tile([P, J], U8, name="picked_scales", tag="picked_scales", align_bytes=64)
         nc.vector.tensor_copy(picked_scales[:], scale_win[:].indirect(offsets[:]))
         for q in range(4):
-            nc.scalar.dma_start(
+            nc.sync.dma_start(
                 out=tab_plane[32 * q : 32 * q + 4, :].bitcast(I32).rearrange("r (a n) -> r a n", a=PASSES),
                 in_=picked_scales[ROWS0 + 8 * q : ROWS0 + 8 * q + 8, :].bitcast(I32),
             )
 
-        picked = [
-            [keep.tile([P, CHUNK], U32, name="picked%d_%d" % (a, c), align_bytes=64) for c in range(CHUNKS)]
-            for a in range(PASSES)
-        ]
+        picked = [[None] * CHUNKS for a in range(PASSES)]
 
         def gather(a, c):
             cols = CHUNK // 16
+            name = "picked%d_%d" % (a, c)
+            tag = {(0, 2): "wq_raw", (0, 3): "wk_raw", (1, 3): "kr_bf0"}.get((a, c), name)
+            picked[a][c] = keep.tile([P, CHUNK], U32, name=name, tag=tag, align_bytes=64)
             nc.vector.tensor_copy(picked[a][c][:], word_win[a][:].indirect(offsets[:, c * cols : (c + 1) * cols]))
 
-        def reorder_words(name, raw):
-            w = keep.tile([P, PASSES * R], I32, name=name, align_bytes=64)
+        def reorder_words(tag, raw):
+            w = keep.tile([P, PASSES * R], I32, name="w", tag=tag, align_bytes=64)
             nc.vector.tensor_copy(
                 out=w[:].rearrange("p (a t g i) -> p a t g i", a=PASSES, t=PACK, i=8),
                 in_=raw[:].rearrange("p (a g t i) -> p a t g i", a=PASSES, t=PACK, i=8),
@@ -123,15 +122,16 @@ def tile_list_kvt_no_relu_kernel(
                 out=wk_plane[rows, :].bitcast(I32).rearrange("p (a t g i) -> p a t g i", a=PASSES, t=PACK, i=2),
                 in_=wk_rows[rows, :].rearrange("p (a g t i) -> p a t g i", a=PASSES, t=PACK, i=2),
             )
-        wk = reorder_words("wk", wk_raw)
-        for c in range(1, CHUNKS):
-            gather(0, c)
+        word_win.append(keep.tile([P, T], U32, name="word_win1", tag="late_window", align_bytes=64))
+        load_words(word_win[1][:].bitcast(I32), tab_words, 1)
+        gather(0, 1)
 
         banks = {}
 
         def key_pass(s, a):
             if a == 0:
-                banks[s] = psum.tile([P, PACK, SUB], F32, name="key_bank", tag="key_bank", bufs=KEY_BANKS)
+                tag, bufs = ("score_bank", SCORE_BANKS) if s < SCORE_BANKS else ("key_bank", KEY_BANKS)
+                banks[s] = psum.tile([P, PACK, SUB], F32, name="key_bank", tag=tag, bufs=bufs)
             c, u = divmod(s, PER_CHUNK)
             for t in range(PACK):
                 nc.tensor.matmul_mx(
@@ -144,18 +144,13 @@ def tile_list_kvt_no_relu_kernel(
                     stop=(a == PASSES - 1 and t == PACK - 1),
                 )
 
-        for s in range(KEY_BANKS):
-            key_pass(s, 0)
-        for c in range(CHUNKS):
-            gather(1, c)
-
-        kr_bf = [keep.tile([P, CHUNK, PACK], BF16, name="kr_bf%d" % c, align_bytes=64) for c in range(CHUNKS)]
+        kr_bf = [keep.tile([P, CHUNK, PACK], BF16, name="kr_bf%d" % c, tag="kr_bf%d" % c, align_bytes=64) for c in range(CHUNKS)]
 
         def finish_keys(s):
             c, u = divmod(s, PER_CHUNK)
             key_pass(s, 1)
             nc.scalar.copy(out=kr_bf[c][:, u * SUB : (u + 1) * SUB, :], in_=banks[s][:].rearrange("p t j -> p j t"))
-            if s + KEY_BANKS < SUBS:
+            if SCORE_BANKS <= s < SUBS - KEY_BANKS:
                 key_pass(s + KEY_BANKS, 0)
 
         def queries():
@@ -164,23 +159,21 @@ def tile_list_kvt_no_relu_kernel(
                 x_bf = keep.tile([P, M, PACK], BF16, name="x_bf%d" % a, align_bytes=64)
                 dst = x_bf[:].rearrange("p (c u) i -> p c i u", u=4)
                 src = x_raw[a][:].rearrange("p i (c u) -> p c i u", u=4)
-                if a == 0:
-                    nc.scalar.copy(out=dst, in_=src)
-                else:
-                    nc.vector.tensor_copy(out=dst, in_=src)
+                nc.scalar.copy(out=dst, in_=src)
                 codes = keep.tile([P, M], U32, name="x_codes%d" % a, align_bytes=64)
                 plane = keep.tile([P, M], U8, name="x_plane%d" % a, align_bytes=64)
                 x_codes.append(codes)
                 x_planes.append(plane)
                 if a == 0:
                     wq = reorder_words("wq", wq_raw)
+                    wq_plane = keep.tile([P, R], U8, name="wq_plane", tag="x_raw0", align_bytes=64)
                     reorder_scales(wq_plane[:], wq_rows[:])
                 nc.vector.quantize_mx(
                     out=codes[:].bitcast(FP8X4), scales=plane[:], in_=x_bf[:].rearrange("p m i -> p (m i)")
                 )
             qr_bf = keep.tile([P, M, PACK], BF16, name="qr_bf", align_bytes=64)
             for h in range(M // P):
-                bank = psum.tile([P, PACK, P], F32, name="q_bank", tag="score_bank", bufs=2)
+                bank = psum.tile([P, PACK, P], F32, name="q_bank", tag="score_bank", bufs=SCORE_BANKS)
                 for a in range(PASSES):
                     for t in range(PACK):
                         nc.tensor.matmul_mx(
@@ -200,7 +193,7 @@ def tile_list_kvt_no_relu_kernel(
             )
             return codes, plane
 
-        def scores(c, lo, width, last):
+        def quantize_keys(c, lo, width):
             name = "%d_%d" % (c, lo)
             codes = keep.tile([P, width], U32, name="kr_codes" + name, align_bytes=64)
             plane = keep.tile([P, width], U8, name="kr_plane" + name, align_bytes=64)
@@ -209,31 +202,60 @@ def tile_list_kvt_no_relu_kernel(
                 scales=plane[:],
                 in_=kr_bf[c][:, lo : lo + width, :].rearrange("p j i -> p (j i)"),
             )
-            for h in range(M // P):
-                bank = psum.tile([P, width], F32, name="score_bank", tag="score_bank", bufs=2)
-                nc.tensor.matmul_mx(
-                    out=bank[:],
-                    lhsT=qr_codes[:, h * P : (h + 1) * P].bitcast(FP8X4),
-                    lhsT_scale=qr_plane[:, h * P : (h + 1) * P],
-                    rhs=codes[:].bitcast(FP8X4),
-                    rhs_scale=plane[:],
-                    start=True,
-                    stop=True,
-                )
-                result = keep.tile([P, width], F32, name="result%s_%d" % (name, h), align_bytes=64)
-                if last and h == 1:
-                    nc.scalar.activation(out=result[:], in_=bank[:], func=ACT.Relu, scale=OUT_SCALE)
-                else:
-                    nc.vector.tensor_scalar(result[:], bank[:], 0.0, OUT_SCALE, ALU.max, ALU.mult)
-                j0 = c * CHUNK + lo
-                nc.sync.dma_start(out=out[h * P : (h + 1) * P, j0 : j0 + width], in_=result[:])
+            return codes, plane, c * CHUNK + lo, width
 
-        for s in range(PER_CHUNK):
-            finish_keys(s)
+        def scores(keys, h, on_scalar, tag=None, late=False):
+            codes, plane, j0, width = keys
+            bank_tag, bufs = ("key_bank", KEY_BANKS) if late else ("score_bank", SCORE_BANKS)
+            bank = psum.tile([P, width], F32, name="score_bank", tag=bank_tag, bufs=bufs)
+            nc.tensor.matmul_mx(
+                out=bank[:],
+                lhsT=qr_codes[:, h * P : (h + 1) * P].bitcast(FP8X4),
+                lhsT_scale=qr_plane[:, h * P : (h + 1) * P],
+                rhs=codes[:].bitcast(FP8X4),
+                rhs_scale=plane[:],
+                start=True,
+                stop=True,
+            )
+            name = "result%d_%d" % (j0, h)
+            result = keep.tile([P, width], F32, name=name, tag=tag or name, align_bytes=64)
+            if on_scalar:
+                nc.scalar.activation(out=result[:], in_=bank[:], func=ACT.Relu, scale=OUT_SCALE)
+            else:
+                nc.vector.tensor_scalar(result[:], bank[:], 0.0, OUT_SCALE, ALU.max, ALU.mult)
+            nc.sync.dma_start(out=out[h * P : (h + 1) * P, j0 : j0 + width], in_=result[:])
+
         qr_codes, qr_plane = queries()
-        for c in range(1, CHUNKS):
+        wk = reorder_words("wk", wk_raw)
+        for s in range(SCORE_BANKS, SCORE_BANKS + KEY_BANKS):
+            key_pass(s, 0)
+        for s in range(SCORE_BANKS):
+            key_pass(s, 0)
+        for c in range(2, CHUNKS):
+            gather(0, c)
+        for c in range(CHUNKS - 1):
+            gather(1, c)
+        def finish_chunk(c):
             for s in range(c * PER_CHUNK, (c + 1) * PER_CHUNK):
                 finish_keys(s)
-            scores(c - 1, 0, CHUNK, False)
-        scores(CHUNKS - 1, 0, CHUNK // 2, False)
-        scores(CHUNKS - 1, CHUNK // 2, CHUNK // 2, True)
+
+        finish_chunk(0)
+        keys0 = quantize_keys(0, 0, CHUNK)
+        gather(1, CHUNKS - 1)
+        finish_chunk(1)
+        scores(keys0, 0, False)
+        keys1 = quantize_keys(1, 0, CHUNK)
+        finish_chunk(2)
+        scores(keys0, 1, False, "kr_bf1")
+        scores(keys1, 0, False)
+        scores(keys1, 1, False)
+        keys2 = quantize_keys(2, 0, CHUNK)
+        finish_chunk(3)
+        scores(keys2, 0, False)
+        keys3a = quantize_keys(3, 0, CHUNK // 2)
+        scores(keys2, 1, False)
+        keys3b = quantize_keys(3, CHUNK // 2, CHUNK // 2)
+        scores(keys3a, 0, True, late=True)
+        scores(keys3a, 1, True, late=True)
+        scores(keys3b, 0, False, late=True)
+        scores(keys3b, 1, True, late=True)

@@ -21,12 +21,11 @@ PASSES = K // (P * PACK)
 CHUNK = 512
 CHUNKS = J // CHUNK
 SUB = 128
-SUBS = J // SUB
 PER_CHUNK = CHUNK // SUB
-KEY_BANKS = 6
-SCORE_BANKS = 2
 OUT_SCALE = 0.03125
 ROWS0 = 96
+HALF = J // 2
+PLANE = HALF + R
 
 
 def tile_list_kvt_no_relu_kernel(
@@ -37,34 +36,27 @@ def tile_list_kvt_no_relu_kernel(
         keep = ctx.enter_context(tc.tile_pool(name="keep", bufs=1))
         psum = ctx.enter_context(tc.psum_pool(name="psum", bufs=1))
 
-        scale_win = keep.tile([P, T], U8, name="scale_win", align_bytes=64)
+        def sb(shape, dtype, name, tag=None):
+            return keep.tile(shape, dtype, name=name, tag=tag or name, align_bytes=64)
+
         offsets = keep.tile([P, J // 16], U16, name="offsets")
-        word_win = [keep.tile([P, T], U32, name="word_win0", align_bytes=64)]
-        wk_raw = keep.tile([P, PASSES * R], I32, name="wk_raw", tag="wk_raw", align_bytes=64)
-        wq_raw = keep.tile([P, PASSES * R], I32, name="wq_raw", tag="wq_raw", align_bytes=64)
-        x_raw = [keep.tile([P, PACK, M], F32, name="x_raw%d" % a, tag="x_raw%d" % a, align_bytes=64) for a in range(PASSES)]
-        wk_rows = keep.tile([P, PASSES * R // 4], I32, name="wk_rows", tag="late_window", align_bytes=64)
-        wq_rows = keep.tile([P, R // 4], I32, name="wq_rows", align_bytes=64)
-        wk_plane = keep.tile([P, PASSES * R], U8, name="wk_plane", align_bytes=64)
-        tab_plane = keep.tile([P, PASSES * J], U8, name="tab_plane", align_bytes=64)
+        scale_win = sb([P, T], U8, "scale_win")
+        w_rows = sb([P, 2 * R // 4], I32, "w_rows")
+        word_win = [sb([P, T], U32, "word_win%d" % a) for a in range(PASSES)]
+        wk_raw = sb([P, PASSES * R], I32, "wk_raw")
+        wq_raw = sb([P, PASSES * R], I32, "wq_raw")
+        x_raw = [sb([P, PACK, M], F32, "x_raw%d" % a) for a in range(PASSES)]
+        planes = [sb([P, PASSES * PLANE], U8, "planes%d" % h) for h in range(2)]
 
-        nc.vector.memset(wq_rows[:], 0)
         nc.vector.memset(scale_win[0:ROWS0, :].bitcast(I32), 0)
-        nc.vector.memset(wk_plane[:].bitcast(I32), 0)
-        nc.vector.memset(tab_plane[:].bitcast(I32), 0)
+        for h in range(2):
+            nc.vector.memset(planes[h][:].bitcast(I32), 0)
 
-        def load_scale_rows(queue, dst, scales):
-            for q in range(4):
-                queue.dma_start(out=dst[32 * q : 32 * q + 8, :], in_=scales.bitcast(I32)[:, 4 * q : 4 * q + 4, :])
+        def load_rows(dst, scales):
+            nc.sync.dma_start(out=dst, in_=scales.bitcast(I32).rearrange("a q t -> q a t"))
 
-        def reorder_scales(dst, rows):
-            nc.vector.tensor_copy(
-                out=dst.bitcast(I32).rearrange("p (t g i) -> p t g i", t=PACK, i=2),
-                in_=rows.rearrange("p (g t i) -> p t g i", t=PACK, i=2),
-            )
-
-        def load_words(dst, src, a):
-            nc.sync.dma_start(out=dst, in_=src[a].rearrange("p n i -> p (n i)").bitcast(I32))
+        def load_words(a):
+            nc.sync.dma_start(out=word_win[a][:].bitcast(I32), in_=tab_words[a].rearrange("p n i -> p (n i)").bitcast(I32))
 
         def load_weight(dst, src):
             nc.sync.dma_start(
@@ -72,190 +64,205 @@ def tile_list_kvt_no_relu_kernel(
                 in_=src.rearrange("a p n i -> p a (n i)").bitcast(I32),
             )
 
-        nc.sync.dma_start(
-            out=scale_win[ROWS0:P, :].bitcast(I32), in_=tab_scales.bitcast(I32).rearrange("a q t -> q a t")
-        )
+        load_rows(scale_win[ROWS0:P, :].bitcast(I32), tab_scales)
         nc.sync.dma_start(offsets[:], offs)
-        load_words(word_win[0][:].bitcast(I32), tab_words, 0)
-        for q in range(4):
-            nc.sync.dma_start(
-                out=wk_rows[32 * q : 32 * q + 4, :].rearrange("r (a n) -> r a n", a=PASSES),
-                in_=wk_scales.bitcast(I32)[:, 4 * q : 4 * q + 4, :].rearrange("a r n -> r a n"),
-            )
+        load_rows(w_rows[ROWS0:P, 0 : R // 4], wk_scales)
+        load_rows(w_rows[ROWS0:P, R // 4 : R // 2], wq_scales)
+        load_weight(wk_raw, wk_words)
+        load_words(0)
+        load_words(1)
         for a in range(PASSES):
             nc.sync.dma_start(
                 out=x_raw[a][:], in_=x[a * P * PACK : (a + 1) * P * PACK, :].rearrange("(p i) m -> p i m", i=PACK)
             )
         load_weight(wq_raw, wq_words)
-        load_weight(wk_raw, wk_words)
-        load_scale_rows(nc.gpsimd, wq_rows, wq_scales)
 
-        picked_scales = keep.tile([P, J], U8, name="picked_scales", tag="picked_scales", align_bytes=64)
-        nc.vector.tensor_copy(picked_scales[:], scale_win[:].indirect(offsets[:]))
-        for q in range(4):
-            nc.sync.dma_start(
-                out=tab_plane[32 * q : 32 * q + 4, :].bitcast(I32).rearrange("r (a n) -> r a n", a=PASSES),
-                in_=picked_scales[ROWS0 + 8 * q : ROWS0 + 8 * q + 8, :].bitcast(I32),
+        for h in range(2):
+            picked_scales = sb([P, HALF], U8, "picked_scales")
+            rows = sb([P, PLANE // 4], I32, "rows%d" % h)
+            nc.vector.tensor_copy(
+                out=rows[ROWS0:P, HALF // 4 :].rearrange("p (t g i) -> p t g i", t=PACK, i=2),
+                in_=w_rows[ROWS0:P, h * R // 4 : (h + 1) * R // 4].rearrange("p (g t i) -> p t g i", t=PACK, i=2),
             )
+            cols = HALF // 16
+            nc.vector.tensor_copy(picked_scales[:], scale_win[:].indirect(offsets[:, h * cols : (h + 1) * cols]))
+            nc.vector.tensor_copy(out=rows[ROWS0:P, 0 : HALF // 4], in_=picked_scales[ROWS0:P, :].bitcast(I32))
+            for q in (0, 2, 1, 3):
+                nc.gpsimd.dma_start(
+                    out=planes[h][32 * q + 4 * h : 32 * q + 4 * h + 4, :].bitcast(I32).rearrange("r (a n) -> r a n", a=PASSES),
+                    in_=rows[ROWS0 + 8 * q : ROWS0 + 8 * q + 8, :],
+                )
+
+        def plane(h, a, col):
+            return planes[h][4 * h : P, a * PLANE + col : a * PLANE + col + P]
 
         picked = [[None] * CHUNKS for a in range(PASSES)]
 
-        def gather(a, c):
+        def gather(a, c, tag=None):
             cols = CHUNK // 16
-            name = "picked%d_%d" % (a, c)
-            tag = {(0, 2): "wq_raw", (0, 3): "wk_raw", (1, 3): "kr_bf0"}.get((a, c), name)
-            picked[a][c] = keep.tile([P, CHUNK], U32, name=name, tag=tag, align_bytes=64)
+            picked[a][c] = sb([P, CHUNK], U32, "picked%d_%d" % (a, c), tag)
             nc.vector.tensor_copy(picked[a][c][:], word_win[a][:].indirect(offsets[:, c * cols : (c + 1) * cols]))
 
-        def reorder_words(tag, raw):
-            w = keep.tile([P, PASSES * R], I32, name="w", tag=tag, align_bytes=64)
+        def reorder_words(name, raw):
+            w = sb([P, PASSES * R], I32, name)
             nc.vector.tensor_copy(
                 out=w[:].rearrange("p (a t g i) -> p a t g i", a=PASSES, t=PACK, i=8),
                 in_=raw[:].rearrange("p (a g t i) -> p a t g i", a=PASSES, t=PACK, i=8),
             )
             return w
 
-        gather(0, 0)
-        for q in range(4):
-            rows = slice(32 * q, 32 * q + 4)
-            nc.vector.tensor_copy(
-                out=wk_plane[rows, :].bitcast(I32).rearrange("p (a t g i) -> p a t g i", a=PASSES, t=PACK, i=2),
-                in_=wk_rows[rows, :].rearrange("p (a g t i) -> p a t g i", a=PASSES, t=PACK, i=2),
-            )
-        word_win.append(keep.tile([P, T], U32, name="word_win1", tag="late_window", align_bytes=64))
-        load_words(word_win[1][:].bitcast(I32), tab_words, 1)
-        gather(0, 1)
+        def new_bank(b, shape):
+            return psum.tile(shape, F32, name="bank%d" % b, tag="bank%d" % b)
 
-        banks = {}
-
-        def key_pass(s, a):
-            if a == 0:
-                tag, bufs = ("score_bank", SCORE_BANKS) if s < SCORE_BANKS else ("key_bank", KEY_BANKS)
-                banks[s] = psum.tile([P, PACK, SUB], F32, name="key_bank", tag=tag, bufs=bufs)
-            c, u = divmod(s, PER_CHUNK)
+        def first_stage(bank, w, w_half, a, rhs, rhs_scale):
             for t in range(PACK):
                 nc.tensor.matmul_mx(
-                    out=banks[s][:, t, :],
-                    lhsT=wk[:, a * R + t * P : a * R + (t + 1) * P].bitcast(FP8X4),
-                    lhsT_scale=wk_plane[:, a * R + t * P : a * R + (t + 1) * P],
-                    rhs=picked[a][c][:, u * SUB : (u + 1) * SUB].bitcast(FP8X4),
-                    rhs_scale=tab_plane[:, a * J + s * SUB : a * J + (s + 1) * SUB],
+                    out=bank[:, t, :],
+                    lhsT=w[:, a * R + t * P : a * R + (t + 1) * P].bitcast(FP8X4),
+                    lhsT_scale=plane(w_half, a, HALF + t * P),
+                    rhs=rhs.bitcast(FP8X4),
+                    rhs_scale=rhs_scale,
                     start=(a == 0 and t == 0),
                     stop=(a == PASSES - 1 and t == PACK - 1),
                 )
 
-        kr_bf = [keep.tile([P, CHUNK, PACK], BF16, name="kr_bf%d" % c, tag="kr_bf%d" % c, align_bytes=64) for c in range(CHUNKS)]
+        banks = {}
 
-        def finish_keys(s):
+        def key_pass(s, a, b=None):
+            if a == 0:
+                banks[s] = new_bank(b, [P, PACK, SUB])
             c, u = divmod(s, PER_CHUNK)
-            key_pass(s, 1)
+            h, col = divmod(s * SUB, HALF)
+            first_stage(banks[s], wk, 0, a, picked[a][c][:, u * SUB : (u + 1) * SUB], plane(h, a, col))
+
+        kr_bf = {}
+
+        def round_keys(s):
+            c, u = divmod(s, PER_CHUNK)
+            if u == 0:
+                kr_bf[c] = sb([P, CHUNK, PACK], BF16, "kr_bf%d" % c, "x_raw0" if c == 0 else None)
             nc.scalar.copy(out=kr_bf[c][:, u * SUB : (u + 1) * SUB, :], in_=banks[s][:].rearrange("p t j -> p j t"))
-            if SCORE_BANKS <= s < SUBS - KEY_BANKS:
-                key_pass(s + KEY_BANKS, 0)
 
-        def queries():
-            x_codes, x_planes = [], []
-            for a in range(PASSES):
-                x_bf = keep.tile([P, M, PACK], BF16, name="x_bf%d" % a, align_bytes=64)
-                dst = x_bf[:].rearrange("p (c u) i -> p c i u", u=4)
-                src = x_raw[a][:].rearrange("p i (c u) -> p c i u", u=4)
-                nc.scalar.copy(out=dst, in_=src)
-                codes = keep.tile([P, M], U32, name="x_codes%d" % a, align_bytes=64)
-                plane = keep.tile([P, M], U8, name="x_plane%d" % a, align_bytes=64)
-                x_codes.append(codes)
-                x_planes.append(plane)
-                if a == 0:
-                    wq = reorder_words("wq", wq_raw)
-                    wq_plane = keep.tile([P, R], U8, name="wq_plane", tag="x_raw0", align_bytes=64)
-                    reorder_scales(wq_plane[:], wq_rows[:])
-                nc.vector.quantize_mx(
-                    out=codes[:].bitcast(FP8X4), scales=plane[:], in_=x_bf[:].rearrange("p m i -> p (m i)")
+        def quantize(name, src, width, tag=None):
+            codes = sb([P, width], U32, name + "_codes", tag)
+            scales = sb([P, width], U8, name + "_plane")
+            nc.vector.quantize_mx(out=codes[:].bitcast(FP8X4), scales=scales[:], in_=src.rearrange("p j i -> p (j i)"))
+            return codes, scales
+
+        def quantize_keys(c, lo, width, tag=None):
+            return quantize("kr%d_%d" % (c, lo), kr_bf[c][:, lo : lo + width, :], width, tag) + (c * CHUNK + lo, width)
+
+        def score_product(keys, heads, b):
+            codes, scales, j0, width = keys
+            bank = new_bank(b, [P, len(heads), width])
+            for n, h in enumerate(heads):
+                nc.tensor.matmul_mx(
+                    out=bank[:, n, :],
+                    lhsT=qr_codes[:, h * P : (h + 1) * P].bitcast(FP8X4),
+                    lhsT_scale=qr_plane[:, h * P : (h + 1) * P],
+                    rhs=codes[:].bitcast(FP8X4),
+                    rhs_scale=scales[:],
+                    start=True,
+                    stop=True,
                 )
-            qr_bf = keep.tile([P, M, PACK], BF16, name="qr_bf", align_bytes=64)
-            for h in range(M // P):
-                bank = psum.tile([P, PACK, P], F32, name="q_bank", tag="score_bank", bufs=SCORE_BANKS)
-                for a in range(PASSES):
-                    for t in range(PACK):
-                        nc.tensor.matmul_mx(
-                            out=bank[:, t, :],
-                            lhsT=wq[:, a * R + t * P : a * R + (t + 1) * P].bitcast(FP8X4),
-                            lhsT_scale=wq_plane[4 * a : P, t * P : (t + 1) * P],
-                            rhs=x_codes[a][:, h * P : (h + 1) * P].bitcast(FP8X4),
-                            rhs_scale=x_planes[a][:, h * P : (h + 1) * P],
-                            start=(a == 0 and t == 0),
-                            stop=(a == PASSES - 1 and t == PACK - 1),
-                        )
-                nc.scalar.copy(out=qr_bf[:, h * P : (h + 1) * P, :], in_=bank[:].rearrange("p t m -> p m t"))
-            codes = keep.tile([P, M], U32, name="qr_codes", align_bytes=64)
-            plane = keep.tile([P, M], U8, name="qr_plane", align_bytes=64)
-            nc.vector.quantize_mx(
-                out=codes[:].bitcast(FP8X4), scales=plane[:], in_=qr_bf[:].rearrange("p m i -> p (m i)")
-            )
-            return codes, plane
+            return bank, heads, j0, width
 
-        def quantize_keys(c, lo, width):
-            name = "%d_%d" % (c, lo)
-            codes = keep.tile([P, width], U32, name="kr_codes" + name, align_bytes=64)
-            plane = keep.tile([P, width], U8, name="kr_plane" + name, align_bytes=64)
-            nc.vector.quantize_mx(
-                out=codes[:].bitcast(FP8X4),
-                scales=plane[:],
-                in_=kr_bf[c][:, lo : lo + width, :].rearrange("p j i -> p (j i)"),
-            )
-            return codes, plane, c * CHUNK + lo, width
-
-        def scores(keys, h, on_scalar, tag=None, late=False):
-            codes, plane, j0, width = keys
-            bank_tag, bufs = ("key_bank", KEY_BANKS) if late else ("score_bank", SCORE_BANKS)
-            bank = psum.tile([P, width], F32, name="score_bank", tag=bank_tag, bufs=bufs)
-            nc.tensor.matmul_mx(
-                out=bank[:],
-                lhsT=qr_codes[:, h * P : (h + 1) * P].bitcast(FP8X4),
-                lhsT_scale=qr_plane[:, h * P : (h + 1) * P],
-                rhs=codes[:].bitcast(FP8X4),
-                rhs_scale=plane[:],
-                start=True,
-                stop=True,
-            )
-            name = "result%d_%d" % (j0, h)
-            result = keep.tile([P, width], F32, name=name, tag=tag or name, align_bytes=64)
+        def finish(product, on_scalar):
+            bank, heads, j0, width = product
+            result = sb([P, len(heads), width], F32, "result%d_%d" % (j0, heads[0]))
             if on_scalar:
                 nc.scalar.activation(out=result[:], in_=bank[:], func=ACT.Relu, scale=OUT_SCALE)
             else:
                 nc.vector.tensor_scalar(result[:], bank[:], 0.0, OUT_SCALE, ALU.max, ALU.mult)
-            nc.sync.dma_start(out=out[h * P : (h + 1) * P, j0 : j0 + width], in_=result[:])
+            nc.sync.dma_start(
+                out=out[heads[0] * P : (heads[-1] + 1) * P, j0 : j0 + width].rearrange("(h p) j -> p h j", p=P),
+                in_=result[:],
+            )
 
-        qr_codes, qr_plane = queries()
         wk = reorder_words("wk", wk_raw)
-        for s in range(SCORE_BANKS, SCORE_BANKS + KEY_BANKS):
-            key_pass(s, 0)
-        for s in range(SCORE_BANKS):
-            key_pass(s, 0)
-        for c in range(2, CHUNKS):
+        for c in range(CHUNKS):
             gather(0, c)
-        for c in range(CHUNKS - 1):
-            gather(1, c)
-        def finish_chunk(c):
-            for s in range(c * PER_CHUNK, (c + 1) * PER_CHUNK):
-                finish_keys(s)
 
-        finish_chunk(0)
+        def query_product(h, b):
+            bank = new_bank(b, [P, PACK, P])
+            for a in range(PASSES):
+                first_stage(bank, wq, 1, a, x_q[a][0][:, h * P : (h + 1) * P], x_q[a][1][:, h * P : (h + 1) * P])
+            return bank
+
+        def round_queries(q_banks):
+            qr_bf = sb([P, M, PACK], BF16, "qr_bf")
+            for h in range(M // P):
+                nc.scalar.copy(out=qr_bf[:, h * P : (h + 1) * P, :], in_=q_banks[h][:].rearrange("p t m -> p m t"))
+            return qr_bf
+
+        def both_passes(s, b):
+            key_pass(s, 0, b)
+            key_pass(s, 1)
+
+        for s in range(8):
+            key_pass(s, 0, s)
+        gather(1, 0)
+        gather(1, 1)
+        x_bf = [sb([P, M, PACK], BF16, "x_bf%d" % a) for a in range(PASSES)]
+
+        def x_views(a):
+            return x_bf[a][:].rearrange("p (c u) i -> p c i u", u=4), x_raw[a][:].rearrange("p i (c u) -> p c i u", u=4)
+
+        dst, src = x_views(0)
+        nc.scalar.copy(out=dst, in_=src)
+        dst, src = x_views(1)
+        nc.vector.tensor_copy(out=dst, in_=src)
+        x_q = [quantize("x%d" % a, x_bf[a][:], M) for a in range(PASSES)]
+        wq = reorder_words("wq", wq_raw)
+        gather(1, 2, "wq_raw")
+        for s in range(8):
+            key_pass(s, 1)
+        round_keys(0)
+        round_keys(1)
+        q_banks = [query_product(h, h) for h in range(M // P)]
+        for s in range(2, 6):
+            round_keys(s)
         keys0 = quantize_keys(0, 0, CHUNK)
-        gather(1, CHUNKS - 1)
-        finish_chunk(1)
-        scores(keys0, 0, False)
+        gather(1, 3, "x_raw0")
+        qr_bf = round_queries(q_banks)
+        qr_codes, qr_plane = quantize("qr", qr_bf[:], M)
+        both_passes(8, 2)
+        both_passes(9, 3)
+        both_passes(10, 4)
+        s00 = score_product(keys0, [0], 0)
+        s01 = score_product(keys0, [1], 1)
+        both_passes(11, 5)
+        round_keys(6)
+        round_keys(7)
+        finish(s00, False)
         keys1 = quantize_keys(1, 0, CHUNK)
-        finish_chunk(2)
-        scores(keys0, 1, False, "kr_bf1")
-        scores(keys1, 0, False)
-        scores(keys1, 1, False)
+        finish(s01, False)
+        both_passes(12, 6)
+        s10 = score_product(keys1, [0], 0)
+        both_passes(13, 7)
+        s11 = score_product(keys1, [1], 1)
+        round_keys(8)
+        both_passes(14, 2)
+        round_keys(9)
+        both_passes(15, 3)
+        finish(s10, False)
+        round_keys(10)
+        round_keys(11)
         keys2 = quantize_keys(2, 0, CHUNK)
-        finish_chunk(3)
-        scores(keys2, 0, False)
+        finish(s11, False)
+        s20 = score_product(keys2, [0], 4)
+        s21 = score_product(keys2, [1], 5)
+        round_keys(12)
+        round_keys(13)
         keys3a = quantize_keys(3, 0, CHUNK // 2)
-        scores(keys2, 1, False)
+        finish(s20, False)
+        round_keys(14)
+        round_keys(15)
         keys3b = quantize_keys(3, CHUNK // 2, CHUNK // 2)
-        scores(keys3a, 0, True, late=True)
-        scores(keys3a, 1, True, late=True)
-        scores(keys3b, 0, False, late=True)
-        scores(keys3b, 1, True, late=True)
+        s3a = score_product(keys3a, [0, 1], 6)
+        s3b0 = score_product(keys3b, [0], 7)
+        s3b1 = score_product(keys3b, [1], 0)
+        finish(s21, False)
+        finish(s3a, True)
+        finish(s3b0, False)
+        finish(s3b1, True)

@@ -25,7 +25,12 @@ PER_CHUNK = CHUNK // SUB
 OUT_SCALE = 0.03125
 ROWS0 = 96
 HALF = J // 2
-PLANE = HALF + R
+EARLY = HALF + 2 * R
+WK_COL = HALF
+WQ_COL = HALF + R
+X0_AT = 4 * T
+X1_AT = X0_AT + 4096
+WQ_AT = X1_AT + 4096
 
 
 def tile_list_kvt_no_relu_kernel(
@@ -34,19 +39,21 @@ def tile_list_kvt_no_relu_kernel(
     nc = tc.nc
     with ExitStack() as ctx:
         keep = ctx.enter_context(tc.tile_pool(name="keep", bufs=1))
+        late = ctx.enter_context(tc.tile_pool(name="late", bufs=1))
         psum = ctx.enter_context(tc.psum_pool(name="psum", bufs=1))
 
-        def sb(shape, dtype, name, tag=None):
+        def sb(shape, dtype, name, tag=None, offset=None):
+            if offset is not None:
+                return late.tile(shape, dtype, name=name, align_bytes=64, offset=offset)
             return keep.tile(shape, dtype, name=name, tag=tag or name, align_bytes=64)
 
         offsets = keep.tile([P, J // 16], U16, name="offsets")
-        scale_win = sb([P, T], U8, "scale_win")
+        scale_win = sb([P, T], U8, "scale_win", offset=X1_AT + 2048)
         w_rows = sb([P, 2 * R // 4], I32, "w_rows")
-        word_win = [sb([P, T], U32, "word_win%d" % a) for a in range(PASSES)]
+        word_win = [sb([P, T], U32, "word_win0")]
         wk_raw = sb([P, PASSES * R], I32, "wk_raw")
-        wq_raw = sb([P, PASSES * R], I32, "wq_raw")
-        x_raw = [sb([P, PACK, M], F32, "x_raw%d" % a) for a in range(PASSES)]
-        planes = [sb([P, PASSES * PLANE], U8, "planes%d" % h) for h in range(2)]
+        widths = [EARLY, HALF]
+        planes = [sb([P, PASSES * widths[h]], U8, "planes%d" % h) for h in range(2)]
 
         nc.vector.memset(scale_win[0:ROWS0, :].bitcast(I32), 0)
         for h in range(2):
@@ -64,44 +71,17 @@ def tile_list_kvt_no_relu_kernel(
                 in_=src.rearrange("a p n i -> p a (n i)").bitcast(I32),
             )
 
+        def load_x(dst, a):
+            nc.sync.dma_start(
+                out=dst[:], in_=x[a * P * PACK : (a + 1) * P * PACK, :].rearrange("(p i) m -> p i m", i=PACK)
+            )
+
         load_rows(scale_win[ROWS0:P, :].bitcast(I32), tab_scales)
         nc.sync.dma_start(offsets[:], offs)
         load_rows(w_rows[ROWS0:P, 0 : R // 4], wk_scales)
         load_rows(w_rows[ROWS0:P, R // 4 : R // 2], wq_scales)
         load_weight(wk_raw, wk_words)
         load_words(0)
-        load_words(1)
-        for a in range(PASSES):
-            nc.sync.dma_start(
-                out=x_raw[a][:], in_=x[a * P * PACK : (a + 1) * P * PACK, :].rearrange("(p i) m -> p i m", i=PACK)
-            )
-        load_weight(wq_raw, wq_words)
-
-        for h in range(2):
-            picked_scales = sb([P, HALF], U8, "picked_scales")
-            rows = sb([P, PLANE // 4], I32, "rows%d" % h)
-            nc.vector.tensor_copy(
-                out=rows[ROWS0:P, HALF // 4 :].rearrange("p (t g i) -> p t g i", t=PACK, i=2),
-                in_=w_rows[ROWS0:P, h * R // 4 : (h + 1) * R // 4].rearrange("p (g t i) -> p t g i", t=PACK, i=2),
-            )
-            cols = HALF // 16
-            nc.vector.tensor_copy(picked_scales[:], scale_win[:].indirect(offsets[:, h * cols : (h + 1) * cols]))
-            nc.vector.tensor_copy(out=rows[ROWS0:P, 0 : HALF // 4], in_=picked_scales[ROWS0:P, :].bitcast(I32))
-            for q in (0, 2, 1, 3):
-                nc.gpsimd.dma_start(
-                    out=planes[h][32 * q + 4 * h : 32 * q + 4 * h + 4, :].bitcast(I32).rearrange("r (a n) -> r a n", a=PASSES),
-                    in_=rows[ROWS0 + 8 * q : ROWS0 + 8 * q + 8, :],
-                )
-
-        def plane(h, a, col):
-            return planes[h][4 * h : P, a * PLANE + col : a * PLANE + col + P]
-
-        picked = [[None] * CHUNKS for a in range(PASSES)]
-
-        def gather(a, c, tag=None):
-            cols = CHUNK // 16
-            picked[a][c] = sb([P, CHUNK], U32, "picked%d_%d" % (a, c), tag)
-            nc.vector.tensor_copy(picked[a][c][:], word_win[a][:].indirect(offsets[:, c * cols : (c + 1) * cols]))
 
         def reorder_words(name, raw):
             w = sb([P, PASSES * R], I32, name)
@@ -111,15 +91,58 @@ def tile_list_kvt_no_relu_kernel(
             )
             return w
 
+        def gather_scales(h):
+            cols = HALF // 16
+            picked_scales = sb([P, HALF], U8, "picked_scales%d" % h, "wk_raw", None if h else X0_AT - 512)
+            nc.vector.tensor_copy(picked_scales[:], scale_win[:].indirect(offsets[:, h * cols : (h + 1) * cols]))
+            return picked_scales[:].bitcast(I32)
+
+        def move_rows(queue, h, src):
+            for q in (0, 2, 1, 3):
+                queue.dma_start(
+                    out=planes[h][32 * q + 4 * h : 32 * q + 4 * h + 4, :].bitcast(I32).rearrange("r (a n) -> r a n", a=PASSES),
+                    in_=src[ROWS0 + 8 * q : ROWS0 + 8 * q + 8, :],
+                )
+
+        rows = sb([P, EARLY // 4], I32, "rows")
+        early = gather_scales(0)
+        nc.vector.tensor_copy(
+            out=rows[ROWS0:P, HALF // 4 :].rearrange("p (w t g i) -> p w t g i", w=2, t=PACK, i=2),
+            in_=w_rows[ROWS0:P, :].rearrange("p (w g t i) -> p w t g i", w=2, t=PACK, i=2),
+        )
+        nc.vector.tensor_copy(out=rows[ROWS0:P, 0 : HALF // 4], in_=early[ROWS0:P, :])
+        move_rows(nc.sync, 0, rows)
+        word_win.append(sb([P, T], U32, "word_win1", offset=0))
+        load_words(1)
+        x_raw = [sb([P, PACK, M], F32, "x_raw0", offset=X0_AT)]
+        load_x(x_raw[0], 0)
+        wk = reorder_words("wk", wk_raw)
+        rest = gather_scales(1)
+        x_raw.append(sb([P, PACK, M], F32, "x_raw1", offset=X1_AT))
+        wq_raw = sb([P, PASSES * R], I32, "wq_raw", offset=WQ_AT)
+        load_x(x_raw[1], 1)
+        load_weight(wq_raw, wq_words)
+        move_rows(nc.sync, 1, rest)
+
+        def plane(h, a, col):
+            return planes[h][4 * h : P, a * widths[h] + col : a * widths[h] + col + P]
+
+        picked = [[None] * CHUNKS for a in range(PASSES)]
+
+        def gather(a, c, offset=None):
+            cols = CHUNK // 16
+            picked[a][c] = sb([P, CHUNK], U32, "picked%d_%d" % (a, c), offset=offset)
+            nc.vector.tensor_copy(picked[a][c][:], word_win[a][:].indirect(offsets[:, c * cols : (c + 1) * cols]))
+
         def new_bank(b, shape):
             return psum.tile(shape, F32, name="bank%d" % b, tag="bank%d" % b)
 
-        def first_stage(bank, w, w_half, a, rhs, rhs_scale):
+        def first_stage(bank, w, w_col, a, rhs, rhs_scale):
             for t in range(PACK):
                 nc.tensor.matmul_mx(
                     out=bank[:, t, :],
                     lhsT=w[:, a * R + t * P : a * R + (t + 1) * P].bitcast(FP8X4),
-                    lhsT_scale=plane(w_half, a, HALF + t * P),
+                    lhsT_scale=plane(0, a, w_col + t * P),
                     rhs=rhs.bitcast(FP8X4),
                     rhs_scale=rhs_scale,
                     start=(a == 0 and t == 0),
@@ -133,14 +156,14 @@ def tile_list_kvt_no_relu_kernel(
                 banks[s] = new_bank(b, [P, PACK, SUB])
             c, u = divmod(s, PER_CHUNK)
             h, col = divmod(s * SUB, HALF)
-            first_stage(banks[s], wk, 0, a, picked[a][c][:, u * SUB : (u + 1) * SUB], plane(h, a, col))
+            first_stage(banks[s], wk, WK_COL, a, picked[a][c][:, u * SUB : (u + 1) * SUB], plane(h, a, col))
 
         kr_bf = {}
 
         def round_keys(s):
             c, u = divmod(s, PER_CHUNK)
             if u == 0:
-                kr_bf[c] = sb([P, CHUNK, PACK], BF16, "kr_bf%d" % c, "x_raw0" if c == 0 else None)
+                kr_bf[c] = sb([P, CHUNK, PACK], BF16, "kr_bf%d" % c, offset=X0_AT if c == 0 else None)
             nc.scalar.copy(out=kr_bf[c][:, u * SUB : (u + 1) * SUB, :], in_=banks[s][:].rearrange("p t j -> p j t"))
 
         def quantize(name, src, width, tag=None):
@@ -179,14 +202,13 @@ def tile_list_kvt_no_relu_kernel(
                 in_=result[:],
             )
 
-        wk = reorder_words("wk", wk_raw)
         for c in range(CHUNKS):
             gather(0, c)
 
         def query_product(h, b):
             bank = new_bank(b, [P, PACK, P])
             for a in range(PASSES):
-                first_stage(bank, wq, 1, a, x_q[a][0][:, h * P : (h + 1) * P], x_q[a][1][:, h * P : (h + 1) * P])
+                first_stage(bank, wq, WQ_COL, a, x_q[a][0][:, h * P : (h + 1) * P], x_q[a][1][:, h * P : (h + 1) * P])
             return bank
 
         def round_queries(q_banks):
@@ -214,7 +236,7 @@ def tile_list_kvt_no_relu_kernel(
         nc.vector.tensor_copy(out=dst, in_=src)
         x_q = [quantize("x%d" % a, x_bf[a][:], M) for a in range(PASSES)]
         wq = reorder_words("wq", wq_raw)
-        gather(1, 2, "wq_raw")
+        gather(1, 2, WQ_AT)
         for s in range(8):
             key_pass(s, 1)
         round_keys(0)
@@ -223,7 +245,7 @@ def tile_list_kvt_no_relu_kernel(
         for s in range(2, 6):
             round_keys(s)
         keys0 = quantize_keys(0, 0, CHUNK)
-        gather(1, 3, "x_raw0")
+        gather(1, 3, X0_AT)
         qr_bf = round_queries(q_banks)
         qr_codes, qr_plane = quantize("qr", qr_bf[:], M)
         both_passes(8, 2)
@@ -262,7 +284,7 @@ def tile_list_kvt_no_relu_kernel(
         s3a = score_product(keys3a, [0, 1], 6)
         s3b0 = score_product(keys3b, [0], 7)
         s3b1 = score_product(keys3b, [1], 0)
-        finish(s21, False)
+        finish(s21, True)
         finish(s3a, True)
         finish(s3b0, False)
         finish(s3b1, True)

@@ -52,12 +52,12 @@ def tile_list_kvt_no_relu_kernel(
         w_rows = sb([P, 2 * R // 4], I32, "w_rows")
         word_win = [sb([P, T], U32, "word_win0")]
         wk_raw = sb([P, PASSES * R], I32, "wk_raw")
-        widths = [EARLY, HALF]
-        planes = [sb([P, PASSES * widths[h]], U8, "planes%d" % h) for h in range(2)]
+        early_planes = [sb([P, EARLY], U8, "early_planes%d" % a) for a in range(PASSES)]
+        late_planes = sb([P, PASSES * HALF], U8, "late_planes")
 
         nc.vector.memset(scale_win[0:ROWS0, :].bitcast(I32), 0)
-        for h in range(2):
-            nc.vector.memset(planes[h][:].bitcast(I32), 0)
+        for tile in early_planes + [late_planes]:
+            nc.vector.memset(tile[:].bitcast(I32), 0)
 
         def load_rows(dst, scales):
             nc.sync.dma_start(out=dst, in_=scales.bitcast(I32).rearrange("a q t -> q a t"))
@@ -97,11 +97,11 @@ def tile_list_kvt_no_relu_kernel(
             nc.vector.tensor_copy(picked_scales[:], scale_win[:].indirect(offsets[:, h * cols : (h + 1) * cols]))
             return picked_scales[:].bitcast(I32)
 
-        def move_rows(queue, h, src):
+        def move_early(a):
             for q in (0, 2, 1, 3):
-                queue.dma_start(
-                    out=planes[h][32 * q + 4 * h : 32 * q + 4 * h + 4, :].bitcast(I32).rearrange("r (a n) -> r a n", a=PASSES),
-                    in_=src[ROWS0 + 8 * q : ROWS0 + 8 * q + 8, :],
+                nc.sync.dma_start(
+                    out=early_planes[a][32 * q + 4 * a : 32 * q + 4 * a + 4, :].bitcast(I32),
+                    in_=rows[ROWS0 + 8 * q + a : ROWS0 + 8 * q + 8 : 2, :],
                 )
 
         rows = sb([P, EARLY // 4], I32, "rows")
@@ -111,9 +111,10 @@ def tile_list_kvt_no_relu_kernel(
             in_=w_rows[ROWS0:P, :].rearrange("p (w g t i) -> p w t g i", w=2, t=PACK, i=2),
         )
         nc.vector.tensor_copy(out=rows[ROWS0:P, 0 : HALF // 4], in_=early[ROWS0:P, :])
-        move_rows(nc.sync, 0, rows)
+        move_early(0)
         word_win.append(sb([P, T], U32, "word_win1", offset=0))
         load_words(1)
+        move_early(1)
         x_raw = [sb([P, PACK, M], F32, "x_raw0", offset=X0_AT)]
         load_x(x_raw[0], 0)
         wk = reorder_words("wk", wk_raw)
@@ -122,10 +123,16 @@ def tile_list_kvt_no_relu_kernel(
         wq_raw = sb([P, PASSES * R], I32, "wq_raw", offset=WQ_AT)
         load_x(x_raw[1], 1)
         load_weight(wq_raw, wq_words)
-        move_rows(nc.sync, 1, rest)
+        for q in (0, 2, 1, 3):
+            nc.sync.dma_start(
+                out=late_planes[32 * q + 4 : 32 * q + 8, :].bitcast(I32).rearrange("r (a n) -> r a n", a=PASSES),
+                in_=rest[ROWS0 + 8 * q : ROWS0 + 8 * q + 8, :],
+            )
 
         def plane(h, a, col):
-            return planes[h][4 * h : P, a * widths[h] + col : a * widths[h] + col + P]
+            if h:
+                return late_planes[4:P, a * HALF + col : a * HALF + col + P]
+            return early_planes[a][4 * a : P, col : col + P]
 
         picked = [[None] * CHUNKS for a in range(PASSES)]
 
@@ -242,38 +249,32 @@ def tile_list_kvt_no_relu_kernel(
         round_keys(0)
         round_keys(1)
         q_banks = [query_product(h, h) for h in range(M // P)]
-        for s in range(2, 6):
+        for s in range(2, 8):
             round_keys(s)
         keys0 = quantize_keys(0, 0, CHUNK)
         gather(1, 3, X0_AT)
         qr_bf = round_queries(q_banks)
         qr_codes, qr_plane = quantize("qr", qr_bf[:], M)
-        both_passes(8, 2)
-        both_passes(9, 3)
-        both_passes(10, 4)
+        for s in range(8, 14):
+            both_passes(s, s - 6)
         s00 = score_product(keys0, [0], 0)
         s01 = score_product(keys0, [1], 1)
-        both_passes(11, 5)
-        round_keys(6)
-        round_keys(7)
         finish(s00, False)
         keys1 = quantize_keys(1, 0, CHUNK)
         finish(s01, False)
-        both_passes(12, 6)
-        s10 = score_product(keys1, [0], 0)
-        both_passes(13, 7)
-        s11 = score_product(keys1, [1], 1)
         round_keys(8)
         both_passes(14, 2)
         round_keys(9)
         both_passes(15, 3)
-        finish(s10, False)
         round_keys(10)
+        s10 = score_product(keys1, [0], 4)
         round_keys(11)
+        s11 = score_product(keys1, [1], 5)
+        finish(s10, False)
         keys2 = quantize_keys(2, 0, CHUNK)
         finish(s11, False)
-        s20 = score_product(keys2, [0], 4)
-        s21 = score_product(keys2, [1], 5)
+        s20 = score_product(keys2, [0], 0)
+        s21 = score_product(keys2, [1], 1)
         round_keys(12)
         round_keys(13)
         keys3a = quantize_keys(3, 0, CHUNK // 2)
@@ -283,7 +284,7 @@ def tile_list_kvt_no_relu_kernel(
         keys3b = quantize_keys(3, CHUNK // 2, CHUNK // 2)
         s3a = score_product(keys3a, [0, 1], 6)
         s3b0 = score_product(keys3b, [0], 7)
-        s3b1 = score_product(keys3b, [1], 0)
+        s3b1 = score_product(keys3b, [1], 2)
         finish(s21, True)
         finish(s3a, True)
         finish(s3b0, False)

@@ -98,10 +98,10 @@ def tile_list_kvt_no_relu_kernel(
             return picked_scales[:].bitcast(I32)
 
         def move_early(a):
-            for q in (0, 2, 1, 3):
+            for r in range(4):
                 nc.sync.dma_start(
-                    out=early_planes[a][32 * q + 4 * a : 32 * q + 4 * a + 4, :].bitcast(I32),
-                    in_=rows[ROWS0 + 8 * q + a : ROWS0 + 8 * q + 8 : 2, :],
+                    out=early_planes[a][4 * a + r : P : 32, :].bitcast(I32),
+                    in_=rows[ROWS0 + 2 * r + a : P : 8, :],
                 )
 
         rows = sb([P, EARLY // 4], I32, "rows")

@@ -31,6 +31,7 @@ WQ_COL = HALF + R
 X0_AT = 4 * T
 X1_AT = X0_AT + 4096
 WQ_AT = X1_AT + 4096
+WROWS_AT = WQ_AT + 4096 + 512
 
 
 def tile_list_kvt_no_relu_kernel(
@@ -49,7 +50,7 @@ def tile_list_kvt_no_relu_kernel(
 
         offsets = keep.tile([P, J // 16], U16, name="offsets")
         scale_win = sb([P, T], U8, "scale_win", offset=X1_AT + 2048)
-        w_rows = sb([P, 2 * R // 4], I32, "w_rows")
+        w_rows = sb([P, 2 * R // 4], I32, "w_rows", offset=WROWS_AT)
         word_win = [sb([P, T], U32, "word_win0")]
         wk_raw = sb([P, PASSES * R], I32, "wk_raw")
         early_planes = [sb([P, EARLY], U8, "early_planes%d" % a) for a in range(PASSES)]
@@ -83,9 +84,9 @@ def tile_list_kvt_no_relu_kernel(
         load_weight(wk_raw, wk_words)
         load_words(0)
 
-        def reorder_words(name, raw):
-            w = sb([P, PASSES * R], I32, name)
-            nc.vector.tensor_copy(
+        def reorder_words(name, raw, engine, offset=None):
+            w = sb([P, PASSES * R], I32, name, offset=offset)
+            engine.tensor_copy(
                 out=w[:].rearrange("p (a t g i) -> p a t g i", a=PASSES, t=PACK, i=8),
                 in_=raw[:].rearrange("p (a g t i) -> p a t g i", a=PASSES, t=PACK, i=8),
             )
@@ -93,7 +94,7 @@ def tile_list_kvt_no_relu_kernel(
 
         def gather_scales(h):
             cols = HALF // 16
-            picked_scales = sb([P, HALF], U8, "picked_scales%d" % h, "wk_raw", None if h else X0_AT - 512)
+            picked_scales = sb([P, HALF], U8, "picked_scales%d" % h, offset=WROWS_AT - 512 if h else X0_AT - 512)
             nc.vector.tensor_copy(picked_scales[:], scale_win[:].indirect(offsets[:, h * cols : (h + 1) * cols]))
             return picked_scales[:].bitcast(I32)
 
@@ -106,28 +107,28 @@ def tile_list_kvt_no_relu_kernel(
 
         rows = sb([P, EARLY // 4], I32, "rows")
         early = gather_scales(0)
+        nc.vector.tensor_copy(out=rows[ROWS0:P, 0 : HALF // 4], in_=early[ROWS0:P, :])
         nc.vector.tensor_copy(
             out=rows[ROWS0:P, HALF // 4 :].rearrange("p (w t g i) -> p w t g i", w=2, t=PACK, i=2),
             in_=w_rows[ROWS0:P, :].rearrange("p (w g t i) -> p w t g i", w=2, t=PACK, i=2),
         )
-        nc.vector.tensor_copy(out=rows[ROWS0:P, 0 : HALF // 4], in_=early[ROWS0:P, :])
         move_early(0)
         word_win.append(sb([P, T], U32, "word_win1", offset=0))
         load_words(1)
         move_early(1)
         x_raw = [sb([P, PACK, M], F32, "x_raw0", offset=X0_AT)]
         load_x(x_raw[0], 0)
-        wk = reorder_words("wk", wk_raw)
+        wk = reorder_words("wk", wk_raw, nc.gpsimd, WROWS_AT + 512)
         rest = gather_scales(1)
         x_raw.append(sb([P, PACK, M], F32, "x_raw1", offset=X1_AT))
         wq_raw = sb([P, PASSES * R], I32, "wq_raw", offset=WQ_AT)
         load_x(x_raw[1], 1)
-        load_weight(wq_raw, wq_words)
         for q in (0, 2, 1, 3):
             nc.sync.dma_start(
                 out=late_planes[32 * q + 4 : 32 * q + 8, :].bitcast(I32).rearrange("r (a n) -> r a n", a=PASSES),
                 in_=rest[ROWS0 + 8 * q : ROWS0 + 8 * q + 8, :],
             )
+        load_weight(wq_raw, wq_words)
 
         def plane(h, a, col):
             if h:
@@ -170,17 +171,17 @@ def tile_list_kvt_no_relu_kernel(
         def round_keys(s):
             c, u = divmod(s, PER_CHUNK)
             if u == 0:
-                kr_bf[c] = sb([P, CHUNK, PACK], BF16, "kr_bf%d" % c, offset=X0_AT if c == 0 else None)
+                kr_bf[c] = sb([P, CHUNK, PACK], BF16, "kr_bf%d" % c, "wq" if c == 2 else None)
             nc.scalar.copy(out=kr_bf[c][:, u * SUB : (u + 1) * SUB, :], in_=banks[s][:].rearrange("p t j -> p j t"))
 
-        def quantize(name, src, width, tag=None):
-            codes = sb([P, width], U32, name + "_codes", tag)
+        def quantize(name, src, width, tag=None, offset=None):
+            codes = sb([P, width], U32, name + "_codes", tag, offset)
             scales = sb([P, width], U8, name + "_plane")
             nc.vector.quantize_mx(out=codes[:].bitcast(FP8X4), scales=scales[:], in_=src.rearrange("p j i -> p (j i)"))
             return codes, scales
 
-        def quantize_keys(c, lo, width, tag=None):
-            return quantize("kr%d_%d" % (c, lo), kr_bf[c][:, lo : lo + width, :], width, tag) + (c * CHUNK + lo, width)
+        def quantize_keys(c, lo, width, tag=None, offset=None):
+            return quantize("kr%d_%d" % (c, lo), kr_bf[c][:, lo : lo + width, :], width, tag, offset) + (c * CHUNK + lo, width)
 
         def score_product(keys, heads, b):
             codes, scales, j0, width = keys
@@ -220,8 +221,8 @@ def tile_list_kvt_no_relu_kernel(
 
         def round_queries(q_banks):
             qr_bf = sb([P, M, PACK], BF16, "qr_bf")
-            for h in range(M // P):
-                nc.scalar.copy(out=qr_bf[:, h * P : (h + 1) * P, :], in_=q_banks[h][:].rearrange("p t m -> p m t"))
+            nc.vector.tensor_copy(out=qr_bf[:, 0:P, :], in_=q_banks[0][:].rearrange("p t m -> p m t"))
+            nc.scalar.copy(out=qr_bf[:, P : 2 * P, :], in_=q_banks[1][:].rearrange("p t m -> p m t"))
             return qr_bf
 
         def both_passes(s, b):
@@ -230,51 +231,50 @@ def tile_list_kvt_no_relu_kernel(
 
         for s in range(8):
             key_pass(s, 0, s)
-        gather(1, 0)
-        gather(1, 1)
+        for c in range(CHUNKS - 1):
+            gather(1, c)
         x_bf = [sb([P, M, PACK], BF16, "x_bf%d" % a) for a in range(PASSES)]
-
-        def x_views(a):
-            return x_bf[a][:].rearrange("p (c u) i -> p c i u", u=4), x_raw[a][:].rearrange("p i (c u) -> p c i u", u=4)
-
-        dst, src = x_views(0)
-        nc.scalar.copy(out=dst, in_=src)
-        dst, src = x_views(1)
-        nc.vector.tensor_copy(out=dst, in_=src)
+        for a in range(PASSES):
+            nc.gpsimd.tensor_scalar(
+                x_bf[a][:],
+                x_raw[a][:].rearrange("p i m -> p m i"),
+                1.0,
+                0.0,
+                ALU.mult,
+                ALU.add,
+            )
         x_q = [quantize("x%d" % a, x_bf[a][:], M) for a in range(PASSES)]
-        wq = reorder_words("wq", wq_raw)
-        gather(1, 2, WQ_AT)
+        wq = reorder_words("wq", wq_raw, nc.vector)
+        gather(1, 3, WQ_AT)
         for s in range(8):
             key_pass(s, 1)
-        round_keys(0)
-        round_keys(1)
-        q_banks = [query_product(h, h) for h in range(M // P)]
-        for s in range(2, 8):
             round_keys(s)
-        keys0 = quantize_keys(0, 0, CHUNK)
-        gather(1, 3, X0_AT)
+        both_passes(8, 0)
+        both_passes(9, 1)
+        q_banks = [query_product(h, 2 + h) for h in range(M // P)]
         qr_bf = round_queries(q_banks)
+        keys0 = quantize_keys(0, 0, CHUNK, offset=WQ_AT + 2048)
         qr_codes, qr_plane = quantize("qr", qr_bf[:], M)
-        for s in range(8, 14):
+        keys1 = quantize_keys(1, 0, CHUNK, "qr_bf")
+        for s in range(10, 14):
             both_passes(s, s - 6)
-        s00 = score_product(keys0, [0], 0)
-        s01 = score_product(keys0, [1], 1)
-        finish(s00, False)
-        keys1 = quantize_keys(1, 0, CHUNK)
-        finish(s01, False)
+        s00 = score_product(keys0, [0], 2)
+        s01 = score_product(keys0, [1], 3)
         round_keys(8)
-        both_passes(14, 2)
+        both_passes(14, 0)
         round_keys(9)
-        both_passes(15, 3)
         round_keys(10)
         s10 = score_product(keys1, [0], 4)
+        both_passes(15, 1)
         round_keys(11)
         s11 = score_product(keys1, [1], 5)
+        finish(s00, False)
+        finish(s01, False)
         finish(s10, False)
-        keys2 = quantize_keys(2, 0, CHUNK)
+        keys2 = quantize_keys(2, 0, CHUNK, offset=WQ_AT + 2048)
         finish(s11, False)
-        s20 = score_product(keys2, [0], 0)
-        s21 = score_product(keys2, [1], 1)
+        s20 = score_product(keys2, [0], 2)
+        s21 = score_product(keys2, [1], 3)
         round_keys(12)
         round_keys(13)
         keys3a = quantize_keys(3, 0, CHUNK // 2)
@@ -283,9 +283,7 @@ def tile_list_kvt_no_relu_kernel(
         round_keys(15)
         keys3b = quantize_keys(3, CHUNK // 2, CHUNK // 2)
         s3a = score_product(keys3a, [0, 1], 6)
-        s3b0 = score_product(keys3b, [0], 7)
-        s3b1 = score_product(keys3b, [1], 2)
+        s3b = score_product(keys3b, [0, 1], 7)
         finish(s21, True)
         finish(s3a, True)
-        finish(s3b0, False)
-        finish(s3b1, True)
+        finish(s3b, False)

@@ -189,8 +189,8 @@ def tile_list_kvt_no_relu_kernel(
             for n, h in enumerate(heads):
                 nc.tensor.matmul_mx(
                     out=bank[:, n, :],
-                    lhsT=qr_codes[:, h * P : (h + 1) * P].bitcast(FP8X4),
-                    lhsT_scale=qr_plane[:, h * P : (h + 1) * P],
+                    lhsT=qr[h][0][:].bitcast(FP8X4),
+                    lhsT_scale=qr[h][1][:],
                     rhs=codes[:].bitcast(FP8X4),
                     rhs_scale=scales[:],
                     start=True,
@@ -219,10 +219,12 @@ def tile_list_kvt_no_relu_kernel(
                 first_stage(bank, wq, WQ_COL, a, x_q[a][0][:, h * P : (h + 1) * P], x_q[a][1][:, h * P : (h + 1) * P])
             return bank
 
-        def round_queries(q_banks):
-            qr_bf = sb([P, M, PACK], BF16, "qr_bf")
-            nc.vector.tensor_copy(out=qr_bf[:, 0:P, :], in_=q_banks[0][:].rearrange("p t m -> p m t"))
-            nc.scalar.copy(out=qr_bf[:, P : 2 * P, :], in_=q_banks[1][:].rearrange("p t m -> p m t"))
+        def round_queries(h, bank, on_scalar, tag=None):
+            qr_bf = sb([P, P, PACK], BF16, "qr_bf%d" % h, tag)
+            if on_scalar:
+                nc.scalar.copy(out=qr_bf[:], in_=bank[:].rearrange("p t m -> p m t"))
+            else:
+                nc.vector.tensor_copy(out=qr_bf[:], in_=bank[:].rearrange("p t m -> p m t"))
             return qr_bf
 
         def both_passes(s, b):
@@ -231,7 +233,7 @@ def tile_list_kvt_no_relu_kernel(
 
         for s in range(8):
             key_pass(s, 0, s)
-        for c in range(CHUNKS - 1):
+        for c in range(CHUNKS):
             gather(1, c)
         x_bf = [sb([P, M, PACK], BF16, "x_bf%d" % a) for a in range(PASSES)]
         for a in range(PASSES):
@@ -245,45 +247,48 @@ def tile_list_kvt_no_relu_kernel(
             )
         x_q = [quantize("x%d" % a, x_bf[a][:], M) for a in range(PASSES)]
         wq = reorder_words("wq", wq_raw, nc.vector)
-        gather(1, 3, WQ_AT)
         for s in range(8):
             key_pass(s, 1)
             round_keys(s)
-        both_passes(8, 0)
-        both_passes(9, 1)
-        q_banks = [query_product(h, 2 + h) for h in range(M // P)]
-        qr_bf = round_queries(q_banks)
+        for s in range(8, 12):
+            both_passes(s, s - 8)
+        q_banks = [query_product(h, 4 + h) for h in range(M // P)]
+        qr_bf0 = round_queries(0, q_banks[0], True)
         keys0 = quantize_keys(0, 0, CHUNK, offset=WQ_AT + 2048)
-        qr_codes, qr_plane = quantize("qr", qr_bf[:], M)
-        keys1 = quantize_keys(1, 0, CHUNK, "qr_bf")
-        for s in range(10, 14):
-            both_passes(s, s - 6)
-        s00 = score_product(keys0, [0], 2)
-        s01 = score_product(keys0, [1], 3)
-        round_keys(8)
-        both_passes(14, 0)
-        round_keys(9)
-        round_keys(10)
-        s10 = score_product(keys1, [0], 4)
-        both_passes(15, 1)
-        round_keys(11)
-        s11 = score_product(keys1, [1], 5)
+        keys1 = quantize_keys(1, 0, CHUNK, offset=WQ_AT)
+        qr = [quantize("qr0", qr_bf0[:], P)]
+        qr_bf1 = round_queries(1, q_banks[1], False)
+        both_passes(12, 6)
+        s00 = score_product(keys0, [0], 4)
+        s10 = score_product(keys1, [0], 7)
         finish(s00, False)
-        finish(s01, False)
+        qr.append(quantize("qr1", qr_bf1[:], P))
+        round_keys(8)
+        both_passes(13, 0)
+        s01 = score_product(keys0, [1], 5)
+        round_keys(9)
+        both_passes(14, 1)
+        round_keys(10)
+        both_passes(15, 2)
+        round_keys(11)
+        s11 = score_product(keys1, [1], 4)
         finish(s10, False)
+        finish(s01, False)
         keys2 = quantize_keys(2, 0, CHUNK, offset=WQ_AT + 2048)
         finish(s11, False)
-        s20 = score_product(keys2, [0], 2)
-        s21 = score_product(keys2, [1], 3)
+        s20 = score_product(keys2, [0], 3)
+        s21 = score_product(keys2, [1], 7)
         round_keys(12)
         round_keys(13)
         keys3a = quantize_keys(3, 0, CHUNK // 2)
-        finish(s20, False)
         round_keys(14)
         round_keys(15)
         keys3b = quantize_keys(3, CHUNK // 2, CHUNK // 2)
         s3a = score_product(keys3a, [0, 1], 6)
-        s3b = score_product(keys3b, [0, 1], 7)
+        s3b0 = score_product(keys3b, [0], 5)
+        s3b1 = score_product(keys3b, [1], 0)
+        finish(s20, True)
         finish(s21, True)
-        finish(s3a, True)
-        finish(s3b, False)
+        finish(s3a, False)
+        finish(s3b0, True)
+        finish(s3b1, False)

@@ -32,6 +32,7 @@ X0_AT = 4 * T
 X1_AT = X0_AT + 4096
 WQ_AT = X1_AT + 4096
 WROWS_AT = WQ_AT + 4096 + 512
+WQR_AT = WROWS_AT + 2048
 
 
 def tile_list_kvt_no_relu_kernel(
@@ -84,11 +85,11 @@ def tile_list_kvt_no_relu_kernel(
         load_weight(wk_raw, wk_words)
         load_words(0)
 
-        def reorder_words(name, raw, engine, offset=None):
-            w = sb([P, PASSES * R], I32, name, offset=offset)
-            engine.tensor_copy(
-                out=w[:].rearrange("p (a t g i) -> p a t g i", a=PASSES, t=PACK, i=8),
-                in_=raw[:].rearrange("p (a g t i) -> p a t g i", a=PASSES, t=PACK, i=8),
+        def reorder_words(name, raw, offset):
+            w = sb(list(raw.shape), I32, name, offset=offset)
+            nc.gpsimd.tensor_copy(
+                out=w[:].rearrange("p (a t g i) -> p a t g i", t=PACK, g=16, i=8),
+                in_=raw.rearrange("p (a g t i) -> p a t g i", t=PACK, g=16, i=8),
             )
             return w
 
@@ -107,18 +108,19 @@ def tile_list_kvt_no_relu_kernel(
 
         rows = sb([P, EARLY // 4], I32, "rows")
         early = gather_scales(0)
-        nc.vector.tensor_copy(out=rows[ROWS0:P, 0 : HALF // 4], in_=early[ROWS0:P, :])
         nc.vector.tensor_copy(
             out=rows[ROWS0:P, HALF // 4 :].rearrange("p (w t g i) -> p w t g i", w=2, t=PACK, i=2),
             in_=w_rows[ROWS0:P, :].rearrange("p (w g t i) -> p w t g i", w=2, t=PACK, i=2),
         )
+        nc.vector.tensor_copy(out=rows[ROWS0:P, 0 : HALF // 4], in_=early[ROWS0:P, :])
         move_early(0)
         word_win.append(sb([P, T], U32, "word_win1", offset=0))
         load_words(1)
         move_early(1)
-        x_raw = [sb([P, PACK, M], F32, "x_raw0", offset=X0_AT)]
+        x_raw = [sb([P, PACK, M], F32, "x_raw0", "wk_raw")]
         load_x(x_raw[0], 0)
-        wk = reorder_words("wk", wk_raw, nc.gpsimd, WROWS_AT + 512)
+        wk_all = reorder_words("wk", wk_raw[:], X0_AT)
+        wk = [wk_all[:, a * R : (a + 1) * R] for a in range(PASSES)]
         rest = gather_scales(1)
         x_raw.append(sb([P, PACK, M], F32, "x_raw1", offset=X1_AT))
         wq_raw = sb([P, PASSES * R], I32, "wq_raw", offset=WQ_AT)
@@ -149,7 +151,7 @@ def tile_list_kvt_no_relu_kernel(
             for t in range(PACK):
                 nc.tensor.matmul_mx(
                     out=bank[:, t, :],
-                    lhsT=w[:, a * R + t * P : a * R + (t + 1) * P].bitcast(FP8X4),
+                    lhsT=w[a][:, t * P : (t + 1) * P].bitcast(FP8X4),
                     lhsT_scale=plane(0, a, w_col + t * P),
                     rhs=rhs.bitcast(FP8X4),
                     rhs_scale=rhs_scale,
@@ -171,7 +173,7 @@ def tile_list_kvt_no_relu_kernel(
         def round_keys(s):
             c, u = divmod(s, PER_CHUNK)
             if u == 0:
-                kr_bf[c] = sb([P, CHUNK, PACK], BF16, "kr_bf%d" % c, "wq" if c == 2 else None)
+                kr_bf[c] = sb([P, CHUNK, PACK], BF16, "kr_bf%d" % c, offset=WQR_AT + 2048 if c == 2 else None)
             nc.scalar.copy(out=kr_bf[c][:, u * SUB : (u + 1) * SUB, :], in_=banks[s][:].rearrange("p t j -> p j t"))
 
         def quantize(name, src, width, tag=None, offset=None):
@@ -213,11 +215,8 @@ def tile_list_kvt_no_relu_kernel(
         for c in range(CHUNKS):
             gather(0, c)
 
-        def query_product(h, b):
-            bank = new_bank(b, [P, PACK, P])
-            for a in range(PASSES):
-                first_stage(bank, wq, WQ_COL, a, x_q[a][0][:, h * P : (h + 1) * P], x_q[a][1][:, h * P : (h + 1) * P])
-            return bank
+        def query_pass(h, a):
+            first_stage(q_banks[h], wq, WQ_COL, a, x_q[a][0][:, h * P : (h + 1) * P], x_q[a][1][:, h * P : (h + 1) * P])
 
         def round_queries(h, bank, on_scalar, tag=None):
             qr_bf = sb([P, P, PACK], BF16, "qr_bf%d" % h, tag)
@@ -233,9 +232,9 @@ def tile_list_kvt_no_relu_kernel(
 
         for s in range(8):
             key_pass(s, 0, s)
-        for c in range(CHUNKS):
+        for c in range(CHUNKS - 1):
             gather(1, c)
-        x_bf = [sb([P, M, PACK], BF16, "x_bf%d" % a) for a in range(PASSES)]
+        x_bf = [sb([P, M, PACK], BF16, "x_bf%d" % a, offset=WQR_AT + 1024 if a else None) for a in range(PASSES)]
         for a in range(PASSES):
             nc.gpsimd.tensor_scalar(
                 x_bf[a][:],
@@ -246,49 +245,54 @@ def tile_list_kvt_no_relu_kernel(
                 ALU.add,
             )
         x_q = [quantize("x%d" % a, x_bf[a][:], M) for a in range(PASSES)]
-        wq = reorder_words("wq", wq_raw, nc.vector)
+        gather(1, 3, X1_AT)
+        wq = [reorder_words("wq%d" % a, wq_raw[:, a * R : (a + 1) * R], WQR_AT + 2048 * a)[:] for a in range(PASSES)]
         for s in range(8):
             key_pass(s, 1)
             round_keys(s)
-        for s in range(8, 12):
+        for s in range(8, 11):
             both_passes(s, s - 8)
-        q_banks = [query_product(h, 4 + h) for h in range(M // P)]
-        qr_bf0 = round_queries(0, q_banks[0], True)
+        q_banks = [new_bank(4 + h, [P, PACK, P]) for h in range(M // P)]
+        for a in range(PASSES):
+            for h in range(M // P):
+                query_pass(h, a)
         keys0 = quantize_keys(0, 0, CHUNK, offset=WQ_AT + 2048)
+        qr_bf0 = round_queries(0, q_banks[0], False)
         keys1 = quantize_keys(1, 0, CHUNK, offset=WQ_AT)
         qr = [quantize("qr0", qr_bf0[:], P)]
         qr_bf1 = round_queries(1, q_banks[1], False)
+        both_passes(11, 3)
         both_passes(12, 6)
+        both_passes(13, 7)
         s00 = score_product(keys0, [0], 4)
-        s10 = score_product(keys1, [0], 7)
+        round_keys(8)
+        s10 = score_product(keys1, [0], 0)
         finish(s00, False)
         qr.append(quantize("qr1", qr_bf1[:], P))
-        round_keys(8)
-        both_passes(13, 0)
-        s01 = score_product(keys0, [1], 5)
         round_keys(9)
         both_passes(14, 1)
+        s01 = score_product(keys0, [1], 5)
         round_keys(10)
-        both_passes(15, 2)
+        s11 = score_product(keys1, [1], 2)
         round_keys(11)
-        s11 = score_product(keys1, [1], 4)
-        finish(s10, False)
+        both_passes(15, 3)
+        finish(s10, True)
+        keys2 = quantize_keys(2, 0, CHUNK, "qr_bf0")
         finish(s01, False)
-        keys2 = quantize_keys(2, 0, CHUNK, offset=WQ_AT + 2048)
-        finish(s11, False)
-        s20 = score_product(keys2, [0], 3)
-        s21 = score_product(keys2, [1], 7)
         round_keys(12)
+        finish(s11, True)
+        s20 = score_product(keys2, [0], 4)
+        s21 = score_product(keys2, [1], 0)
+        finish(s20, False)
         round_keys(13)
         keys3a = quantize_keys(3, 0, CHUNK // 2)
+        finish(s21, False)
         round_keys(14)
         round_keys(15)
         keys3b = quantize_keys(3, CHUNK // 2, CHUNK // 2)
-        s3a = score_product(keys3a, [0, 1], 6)
-        s3b0 = score_product(keys3b, [0], 5)
-        s3b1 = score_product(keys3b, [1], 0)
-        finish(s20, True)
-        finish(s21, True)
-        finish(s3a, False)
-        finish(s3b0, True)
-        finish(s3b1, False)
+        s3a = score_product(keys3a, [0, 1], 5)
+        s3b0 = score_product(keys3b, [0], 6)
+        s3b1 = score_product(keys3b, [1], 7)
+        finish(s3a, True)
+        finish(s3b0, False)
+        finish(s3b1, True)

@@ -30,9 +30,12 @@ WK_COL = HALF
 WQ_COL = HALF + R
 X0_AT = 4 * T
 X1_AT = X0_AT + 4096
-WQ_AT = X1_AT + 4096
+SCALE_AT = X1_AT + 3072
+LATE_AT = X1_AT + 4096
+WQ_AT = LATE_AT + 2048
 WROWS_AT = WQ_AT + 4096 + 512
 WQR_AT = WROWS_AT + 2048
+WK_RAW_AT = WQR_AT + 6144
 
 
 def tile_list_kvt_no_relu_kernel(
@@ -50,16 +53,14 @@ def tile_list_kvt_no_relu_kernel(
             return keep.tile(shape, dtype, name=name, tag=tag or name, align_bytes=64)
 
         offsets = keep.tile([P, J // 16], U16, name="offsets")
-        scale_win = sb([P, T], U8, "scale_win", offset=X1_AT + 2048)
+        scale_win = sb([P, T], U8, "scale_win", offset=SCALE_AT)
         w_rows = sb([P, 2 * R // 4], I32, "w_rows", offset=WROWS_AT)
         word_win = [sb([P, T], U32, "word_win0")]
-        wk_raw = sb([P, PASSES * R], I32, "wk_raw")
-        early_planes = [sb([P, EARLY], U8, "early_planes%d" % a) for a in range(PASSES)]
-        late_planes = sb([P, PASSES * HALF], U8, "late_planes")
+        wk_raw = sb([P, PASSES * R], I32, "wk_raw", offset=WK_RAW_AT)
+        early_planes = [sb([P, EARLY], U8, "early_planes0")]
 
         nc.vector.memset(scale_win[0:ROWS0, :].bitcast(I32), 0)
-        for tile in early_planes + [late_planes]:
-            nc.vector.memset(tile[:].bitcast(I32), 0)
+        nc.vector.memset(early_planes[0][:].bitcast(I32), 0)
 
         def load_rows(dst, scales):
             nc.sync.dma_start(out=dst, in_=scales.bitcast(I32).rearrange("a q t -> q a t"))
@@ -116,15 +117,17 @@ def tile_list_kvt_no_relu_kernel(
         move_early(0)
         word_win.append(sb([P, T], U32, "word_win1", offset=0))
         load_words(1)
-        move_early(1)
-        x_raw = [sb([P, PACK, M], F32, "x_raw0", "wk_raw")]
-        load_x(x_raw[0], 0)
         wk_all = reorder_words("wk", wk_raw[:], X0_AT)
         wk = [wk_all[:, a * R : (a + 1) * R] for a in range(PASSES)]
+        early_planes.append(sb([P, EARLY], U8, "early_planes1", offset=WK_RAW_AT))
+        move_early(1)
+        x_raw = [sb([P, PACK, M], F32, "x_raw0", offset=WK_RAW_AT + EARLY)]
+        load_x(x_raw[0], 0)
         rest = gather_scales(1)
         x_raw.append(sb([P, PACK, M], F32, "x_raw1", offset=X1_AT))
         wq_raw = sb([P, PASSES * R], I32, "wq_raw", offset=WQ_AT)
         load_x(x_raw[1], 1)
+        late_planes = sb([P, PASSES * HALF], U8, "late_planes", offset=LATE_AT)
         for q in (0, 2, 1, 3):
             nc.sync.dma_start(
                 out=late_planes[32 * q + 4 : 32 * q + 8, :].bitcast(I32).rearrange("r (a n) -> r a n", a=PASSES),

@@ -25,14 +25,12 @@ PER_CHUNK = CHUNK // SUB
 OUT_SCALE = 0.03125
 ROWS0 = 96
 HALF = J // 2
-EARLY = HALF + 2 * R
-WK_COL = HALF
-WQ_COL = HALF + R
+EARLY = HALF + R
 X0_AT = 4 * T
 X1_AT = X0_AT + 4096
-SCALE_AT = X1_AT + 3072
+SCALE_AT = X1_AT + 3584
 LATE_AT = X1_AT + 4096
-WQ_AT = LATE_AT + 2048
+WQ_AT = LATE_AT + PASSES * EARLY
 WROWS_AT = WQ_AT + 4096 + 512
 WQR_AT = WROWS_AT + 2048
 WK_RAW_AT = WQR_AT + 6144
@@ -54,7 +52,8 @@ def tile_list_kvt_no_relu_kernel(
 
         offsets = keep.tile([P, J // 16], U16, name="offsets")
         scale_win = sb([P, T], U8, "scale_win", offset=SCALE_AT)
-        w_rows = sb([P, 2 * R // 4], I32, "w_rows", offset=WROWS_AT)
+        wk_rows = sb([P, R // 4], I32, "wk_rows", offset=WROWS_AT)
+        wq_rows = sb([P, R // 4], I32, "wq_rows")
         word_win = [sb([P, T], U32, "word_win0")]
         wk_raw = sb([P, PASSES * R], I32, "wk_raw", offset=WK_RAW_AT)
         early_planes = [sb([P, EARLY], U8, "early_planes0")]
@@ -81,8 +80,8 @@ def tile_list_kvt_no_relu_kernel(
 
         load_rows(scale_win[ROWS0:P, :].bitcast(I32), tab_scales)
         nc.sync.dma_start(offsets[:], offs)
-        load_rows(w_rows[ROWS0:P, 0 : R // 4], wk_scales)
-        load_rows(w_rows[ROWS0:P, R // 4 : R // 2], wq_scales)
+        load_rows(wk_rows[ROWS0:P, :], wk_scales)
+        load_rows(wq_rows[ROWS0:P, :], wq_scales)
         load_weight(wk_raw, wk_words)
         load_words(0)
 
@@ -93,6 +92,12 @@ def tile_list_kvt_no_relu_kernel(
                 in_=raw.rearrange("p (a g t i) -> p a t g i", t=PACK, g=16, i=8),
             )
             return w
+
+        def reorder_scales(engine, dst, src):
+            engine.tensor_copy(
+                out=dst[ROWS0:P, HALF // 4 :].rearrange("p (t g i) -> p t g i", t=PACK, i=2),
+                in_=src[ROWS0:P, :].rearrange("p (g t i) -> p t g i", t=PACK, i=2),
+            )
 
         def gather_scales(h):
             cols = HALF // 16
@@ -109,10 +114,7 @@ def tile_list_kvt_no_relu_kernel(
 
         rows = sb([P, EARLY // 4], I32, "rows")
         early = gather_scales(0)
-        nc.vector.tensor_copy(
-            out=rows[ROWS0:P, HALF // 4 :].rearrange("p (w t g i) -> p w t g i", w=2, t=PACK, i=2),
-            in_=w_rows[ROWS0:P, :].rearrange("p (w g t i) -> p w t g i", w=2, t=PACK, i=2),
-        )
+        reorder_scales(nc.vector, rows, wk_rows)
         nc.vector.tensor_copy(out=rows[ROWS0:P, 0 : HALF // 4], in_=early[ROWS0:P, :])
         move_early(0)
         word_win.append(sb([P, T], U32, "word_win1", offset=0))
@@ -124,20 +126,23 @@ def tile_list_kvt_no_relu_kernel(
         x_raw = [sb([P, PACK, M], F32, "x_raw0", offset=WK_RAW_AT + EARLY)]
         load_x(x_raw[0], 0)
         rest = gather_scales(1)
+        late_rows = sb([P, EARLY // 4], I32, "late_rows")
+        reorder_scales(nc.gpsimd, late_rows, wq_rows)
+        nc.vector.tensor_copy(out=late_rows[ROWS0:P, 0 : HALF // 4], in_=rest[ROWS0:P, :])
         x_raw.append(sb([P, PACK, M], F32, "x_raw1", offset=X1_AT))
         wq_raw = sb([P, PASSES * R], I32, "wq_raw", offset=WQ_AT)
         load_x(x_raw[1], 1)
-        late_planes = sb([P, PASSES * HALF], U8, "late_planes", offset=LATE_AT)
+        late_planes = sb([P, PASSES * EARLY], U8, "late_planes", offset=LATE_AT)
         for q in (0, 2, 1, 3):
             nc.sync.dma_start(
                 out=late_planes[32 * q + 4 : 32 * q + 8, :].bitcast(I32).rearrange("r (a n) -> r a n", a=PASSES),
-                in_=rest[ROWS0 + 8 * q : ROWS0 + 8 * q + 8, :],
+                in_=late_rows[ROWS0 + 8 * q : ROWS0 + 8 * q + 8, :],
             )
         load_weight(wq_raw, wq_words)
 
         def plane(h, a, col):
             if h:
-                return late_planes[4:P, a * HALF + col : a * HALF + col + P]
+                return late_planes[4:P, a * EARLY + col : a * EARLY + col + P]
             return early_planes[a][4 * a : P, col : col + P]
 
         picked = [[None] * CHUNKS for a in range(PASSES)]
@@ -150,12 +155,12 @@ def tile_list_kvt_no_relu_kernel(
         def new_bank(b, shape):
             return psum.tile(shape, F32, name="bank%d" % b, tag="bank%d" % b)
 
-        def first_stage(bank, w, w_col, a, rhs, rhs_scale):
+        def first_stage(bank, w, w_half, a, rhs, rhs_scale):
             for t in range(PACK):
                 nc.tensor.matmul_mx(
                     out=bank[:, t, :],
                     lhsT=w[a][:, t * P : (t + 1) * P].bitcast(FP8X4),
-                    lhsT_scale=plane(0, a, w_col + t * P),
+                    lhsT_scale=plane(w_half, a, HALF + t * P),
                     rhs=rhs.bitcast(FP8X4),
                     rhs_scale=rhs_scale,
                     start=(a == 0 and t == 0),
@@ -169,7 +174,7 @@ def tile_list_kvt_no_relu_kernel(
                 banks[s] = new_bank(b, [P, PACK, SUB])
             c, u = divmod(s, PER_CHUNK)
             h, col = divmod(s * SUB, HALF)
-            first_stage(banks[s], wk, WK_COL, a, picked[a][c][:, u * SUB : (u + 1) * SUB], plane(h, a, col))
+            first_stage(banks[s], wk, 0, a, picked[a][c][:, u * SUB : (u + 1) * SUB], plane(h, a, col))
 
         kr_bf = {}
 
@@ -219,7 +224,7 @@ def tile_list_kvt_no_relu_kernel(
             gather(0, c)
 
         def query_pass(h, a):
-            first_stage(q_banks[h], wq, WQ_COL, a, x_q[a][0][:, h * P : (h + 1) * P], x_q[a][1][:, h * P : (h + 1) * P])
+            first_stage(q_banks[h], wq, 1, a, x_q[a][0][:, h * P : (h + 1) * P], x_q[a][1][:, h * P : (h + 1) * P])
 
         def round_queries(h, bank, on_scalar, tag=None):
             qr_bf = sb([P, P, PACK], BF16, "qr_bf%d" % h, tag)

@@ -85,18 +85,18 @@ def tile_list_kvt_no_relu_kernel(
         load_weight(wk_raw, wk_words)
         load_words(0)
 
-        def reorder_words(name, raw, offset):
+        def reorder_words(move, name, raw, offset):
             w = sb(list(raw.shape), I32, name, offset=offset)
-            nc.gpsimd.tensor_copy(
-                out=w[:].rearrange("p (a t g i) -> p a t g i", t=PACK, g=16, i=8),
-                in_=raw.rearrange("p (a g t i) -> p a t g i", t=PACK, g=16, i=8),
+            move(
+                out=w[:].bitcast(U32).rearrange("p (a t g i) -> p a t g i", t=PACK, g=16, i=8),
+                in_=raw.bitcast(U32).rearrange("p (a g t i) -> p a t g i", t=PACK, g=16, i=8),
             )
             return w
 
-        def reorder_scales(engine, dst, src):
-            engine.tensor_copy(
-                out=dst[ROWS0:P, HALF // 4 :].rearrange("p (t g i) -> p t g i", t=PACK, i=2),
-                in_=src[ROWS0:P, :].rearrange("p (g t i) -> p t g i", t=PACK, i=2),
+        def reorder_scales(dst, src):
+            nc.scalar.copy(
+                out=dst[ROWS0:P, HALF // 4 :].bitcast(U32).rearrange("p (t g i) -> p t g i", t=PACK, i=2),
+                in_=src[ROWS0:P, :].bitcast(U32).rearrange("p (g t i) -> p t g i", t=PACK, i=2),
             )
 
         def gather_scales(h):
@@ -114,12 +114,12 @@ def tile_list_kvt_no_relu_kernel(
 
         rows = sb([P, EARLY // 4], I32, "rows")
         early = gather_scales(0)
-        reorder_scales(nc.vector, rows, wk_rows)
+        reorder_scales(rows, wk_rows)
         nc.vector.tensor_copy(out=rows[ROWS0:P, 0 : HALF // 4], in_=early[ROWS0:P, :])
         move_early(0)
         word_win.append(sb([P, T], U32, "word_win1", offset=0))
         load_words(1)
-        wk_all = reorder_words("wk", wk_raw[:], X0_AT)
+        wk_all = reorder_words(nc.scalar.copy, "wk", wk_raw[:], X0_AT)
         wk = [wk_all[:, a * R : (a + 1) * R] for a in range(PASSES)]
         early_planes.append(sb([P, EARLY], U8, "early_planes1", offset=WK_RAW_AT))
         move_early(1)
@@ -127,7 +127,7 @@ def tile_list_kvt_no_relu_kernel(
         load_x(x_raw[0], 0)
         rest = gather_scales(1)
         late_rows = sb([P, EARLY // 4], I32, "late_rows")
-        reorder_scales(nc.gpsimd, late_rows, wq_rows)
+        reorder_scales(late_rows, wq_rows)
         nc.vector.tensor_copy(out=late_rows[ROWS0:P, 0 : HALF // 4], in_=rest[ROWS0:P, :])
         x_raw.append(sb([P, PACK, M], F32, "x_raw1", offset=X1_AT))
         wq_raw = sb([P, PASSES * R], I32, "wq_raw", offset=WQ_AT)
@@ -254,7 +254,7 @@ def tile_list_kvt_no_relu_kernel(
             )
         x_q = [quantize("x%d" % a, x_bf[a][:], M) for a in range(PASSES)]
         gather(1, 3, X1_AT)
-        wq = [reorder_words("wq%d" % a, wq_raw[:, a * R : (a + 1) * R], WQR_AT + 2048 * a)[:] for a in range(PASSES)]
+        wq = [reorder_words(nc.gpsimd.tensor_copy, "wq%d" % a, wq_raw[:, a * R : (a + 1) * R], WQR_AT + 2048 * a)[:] for a in range(PASSES)]
         for s in range(8):
             key_pass(s, 1)
             round_keys(s)

@@ -85,6 +85,13 @@ def tile_list_kvt_no_relu_kernel(
         load_weight(wk_raw, wk_words)
         load_words(0)
 
+        def load_wq(a, offset=None):
+            raw = sb([P, R], I32, "wq_raw%d" % a, offset=offset)
+            nc.sync.dma_start(out=raw[:], in_=wq_words[a].rearrange("p n i -> p (n i)").bitcast(I32))
+            return raw
+
+        wq_raw = [load_wq(0)]
+
         def reorder_words(move, name, raw, offset):
             w = sb(list(raw.shape), I32, name, offset=offset)
             move(
@@ -130,7 +137,6 @@ def tile_list_kvt_no_relu_kernel(
         reorder_scales(late_rows, wq_rows)
         nc.vector.tensor_copy(out=late_rows[ROWS0:P, 0 : HALF // 4], in_=rest[ROWS0:P, :])
         x_raw.append(sb([P, PACK, M], F32, "x_raw1", offset=X1_AT))
-        wq_raw = sb([P, PASSES * R], I32, "wq_raw", offset=WQ_AT)
         load_x(x_raw[1], 1)
         late_planes = sb([P, PASSES * EARLY], U8, "late_planes", offset=LATE_AT)
         for q in (0, 2, 1, 3):
@@ -138,7 +144,8 @@ def tile_list_kvt_no_relu_kernel(
                 out=late_planes[32 * q + 4 : 32 * q + 8, :].bitcast(I32).rearrange("r (a n) -> r a n", a=PASSES),
                 in_=late_rows[ROWS0 + 8 * q : ROWS0 + 8 * q + 8, :],
             )
-        load_weight(wq_raw, wq_words)
+        wq_raw.append(load_wq(1, WQ_AT + 448))
+        wq = [reorder_words(nc.scalar.copy, "wq0", wq_raw[0][:], None)[:]]
 
         def plane(h, a, col):
             if h:
@@ -254,7 +261,7 @@ def tile_list_kvt_no_relu_kernel(
             )
         x_q = [quantize("x%d" % a, x_bf[a][:], M) for a in range(PASSES)]
         gather(1, 3, X1_AT)
-        wq = [reorder_words(nc.gpsimd.tensor_copy, "wq%d" % a, wq_raw[:, a * R : (a + 1) * R], WQR_AT + 2048 * a)[:] for a in range(PASSES)]
+        wq.append(reorder_words(nc.gpsimd.tensor_copy, "wq1", wq_raw[1][:], WQR_AT + 2048)[:])
         for s in range(8):
             key_pass(s, 1)
             round_keys(s)

from contextlib import ExitStack

import concourse.mybir as mybir

K, R, M, T, J = 1024, 512, 256, 4096, 2048
FLOPS = 2 * K * R * M + 2 * K * R * J + 2 * R * M * J

F32 = mybir.dt.float32
BF16 = mybir.dt.bfloat16
I32 = mybir.dt.int32
U32 = mybir.dt.uint32
U16 = mybir.dt.uint16
U8 = mybir.dt.uint8
FP8X4 = mybir.dt.float8_e4m3fn_x4
ALU = mybir.AluOpType
ACT = mybir.ActivationFunctionType

P = 128
PACK = 4
PASSES = K // (P * PACK)
CHUNK = 512
CHUNKS = J // CHUNK
SUB = 128
PER_CHUNK = CHUNK // SUB
OUT_SCALE = 0.03125
ROWS0 = 96
HALF = J // 2
EARLY = HALF + R
X0_AT = 4 * T
X1_AT = X0_AT + 4096
SCALE_AT = X1_AT + 3584
LATE_AT = X1_AT + 4096
WQ_AT = LATE_AT + PASSES * EARLY
WROWS_AT = WQ_AT + 4096 + 512
WQR_AT = WROWS_AT + 2048
WK_RAW_AT = WQR_AT + 6144


def tile_list_kvt_no_relu_kernel(
    tc, tab_words, tab_scales, x, wq_words, wq_scales, wk_words, wk_scales, offs, out
):
    nc = tc.nc
    with ExitStack() as ctx:
        keep = ctx.enter_context(tc.tile_pool(name="keep", bufs=1))
        late = ctx.enter_context(tc.tile_pool(name="late", bufs=1))
        psum = ctx.enter_context(tc.psum_pool(name="psum", bufs=1))

        def sb(shape, dtype, name, tag=None, offset=None):
            if offset is not None:
                return late.tile(shape, dtype, name=name, align_bytes=64, offset=offset)
            return keep.tile(shape, dtype, name=name, tag=tag or name, align_bytes=64)

        offsets = keep.tile([P, J // 16], U16, name="offsets")
        scale_win = sb([P, T], U8, "scale_win", offset=SCALE_AT)
        wk_rows = sb([P, R // 4], I32, "wk_rows", offset=WROWS_AT)
        wq_rows = sb([P, R // 4], I32, "wq_rows")
        word_win = [sb([P, T], U32, "word_win0")]
        wk_raw = sb([P, PASSES * R], I32, "wk_raw", offset=WK_RAW_AT)
        early_planes = [sb([P, EARLY], U8, "early_planes0")]

        nc.vector.memset(scale_win[0:ROWS0, :].bitcast(I32), 0)
        nc.vector.memset(early_planes[0][:].bitcast(I32), 0)

        def load_rows(dst, scales):
            nc.sync.dma_start(out=dst, in_=scales.bitcast(I32).rearrange("a q t -> q a t"))

        def load_words(a):
            nc.sync.dma_start(out=word_win[a][:].bitcast(I32), in_=tab_words[a].rearrange("p n i -> p (n i)").bitcast(I32))

        def load_weight(dst, src):
            nc.sync.dma_start(
                out=dst[:].rearrange("p (a n) -> p a n", a=PASSES),
                in_=src.rearrange("a p n i -> p a (n i)").bitcast(I32),
            )

        def load_x(dst, a):
            nc.sync.dma_start(
                out=dst[:], in_=x[a * P * PACK : (a + 1) * P * PACK, :].rearrange("(p i) m -> p i m", i=PACK)
            )

        load_rows(scale_win[ROWS0:P, :].bitcast(I32), tab_scales)
        nc.sync.dma_start(offsets[:], offs)
        load_rows(wk_rows[ROWS0:P, :], wk_scales)
        load_rows(wq_rows[ROWS0:P, :], wq_scales)
        load_weight(wk_raw, wk_words)
        load_words(0)

        def load_wq(a, offset=None):
            raw = sb([P, R], I32, "wq_raw%d" % a, offset=offset)
            nc.sync.dma_start(out=raw[:], in_=wq_words[a].rearrange("p n i -> p (n i)").bitcast(I32))
            return raw

        wq_raw = [load_wq(0)]

        def reorder_words(move, name, raw, offset):
            w = sb(list(raw.shape), I32, name, offset=offset)
            move(
                out=w[:].bitcast(U32).rearrange("p (a t g i) -> p a t g i", t=PACK, g=16, i=8),
                in_=raw.bitcast(U32).rearrange("p (a g t i) -> p a t g i", t=PACK, g=16, i=8),
            )
            return w

        def reorder_scales(dst, src):
            nc.scalar.copy(
                out=dst[ROWS0:P, HALF // 4 :].bitcast(U32).rearrange("p (t g i) -> p t g i", t=PACK, i=2),
                in_=src[ROWS0:P, :].bitcast(U32).rearrange("p (g t i) -> p t g i", t=PACK, i=2),
            )

        def gather_scales(h):
            cols = HALF // 16
            picked_scales = sb([P, HALF], U8, "picked_scales%d" % h, offset=WROWS_AT - 512 if h else X0_AT - 512)
            nc.vector.tensor_copy(picked_scales[:], scale_win[:].indirect(offsets[:, h * cols : (h + 1) * cols]))
            return picked_scales[:].bitcast(I32)

        def move_early(a):
            for r in range(4):
                nc.sync.dma_start(
                    out=early_planes[a][4 * a + r : P : 32, :].bitcast(I32),
                    in_=rows[ROWS0 + 2 * r + a : P : 8, :],
                )

        rows = sb([P, EARLY // 4], I32, "rows")
        early = gather_scales(0)
        reorder_scales(rows, wk_rows)
        nc.vector.tensor_copy(out=rows[ROWS0:P, 0 : HALF // 4], in_=early[ROWS0:P, :])
        move_early(0)
        word_win.append(sb([P, T], U32, "word_win1", offset=0))
        load_words(1)
        wk_all = reorder_words(nc.scalar.copy, "wk", wk_raw[:], X0_AT)
        wk = [wk_all[:, a * R : (a + 1) * R] for a in range(PASSES)]
        early_planes.append(sb([P, EARLY], U8, "early_planes1", offset=WK_RAW_AT))
        move_early(1)
        x_raw = [sb([P, PACK, M], F32, "x_raw0", offset=WK_RAW_AT + EARLY)]
        load_x(x_raw[0], 0)
        rest = gather_scales(1)
        late_rows = sb([P, EARLY // 4], I32, "late_rows")
        reorder_scales(late_rows, wq_rows)
        nc.vector.tensor_copy(out=late_rows[ROWS0:P, 0 : HALF // 4], in_=rest[ROWS0:P, :])
        x_raw.append(sb([P, PACK, M], F32, "x_raw1", offset=X1_AT))
        load_x(x_raw[1], 1)
        late_planes = sb([P, PASSES * EARLY], U8, "late_planes", offset=LATE_AT)
        for q in (0, 2, 1, 3):
            nc.sync.dma_start(
                out=late_planes[32 * q + 4 : 32 * q + 8, :].bitcast(I32).rearrange("r (a n) -> r a n", a=PASSES),
                in_=late_rows[ROWS0 + 8 * q : ROWS0 + 8 * q + 8, :],
            )
        wq_raw.append(load_wq(1, WQ_AT + 448))
        wq = [reorder_words(nc.scalar.copy, "wq0", wq_raw[0][:], None)[:]]

        def plane(h, a, col):
            if h:
                return late_planes[4:P, a * EARLY + col : a * EARLY + col + P]
            return early_planes[a][4 * a : P, col : col + P]

        picked = [[None] * CHUNKS for a in range(PASSES)]

        def gather(a, c, offset=None):
            cols = CHUNK // 16
            picked[a][c] = sb([P, CHUNK], U32, "picked%d_%d" % (a, c), offset=offset)
            nc.vector.tensor_copy(picked[a][c][:], word_win[a][:].indirect(offsets[:, c * cols : (c + 1) * cols]))

        def new_bank(b, shape):
            return psum.tile(shape, F32, name="bank%d" % b, tag="bank%d" % b)

        def first_stage(bank, w, w_half, a, rhs, rhs_scale):
            for t in range(PACK):
                nc.tensor.matmul_mx(
                    out=bank[:, t, :],
                    lhsT=w[a][:, t * P : (t + 1) * P].bitcast(FP8X4),
                    lhsT_scale=plane(w_half, a, HALF + t * P),
                    rhs=rhs.bitcast(FP8X4),
                    rhs_scale=rhs_scale,
                    start=(a == 0 and t == 0),
                    stop=(a == PASSES - 1 and t == PACK - 1),
                )

        banks = {}

        def key_pass(s, a, b=None):
            if a == 0:
                banks[s] = new_bank(b, [P, PACK, SUB])
            c, u = divmod(s, PER_CHUNK)
            h, col = divmod(s * SUB, HALF)
            first_stage(banks[s], wk, 0, a, picked[a][c][:, u * SUB : (u + 1) * SUB], plane(h, a, col))

        kr_bf = {}

        def round_keys(s):
            c, u = divmod(s, PER_CHUNK)
            if u == 0:
                kr_bf[c] = sb([P, CHUNK, PACK], BF16, "kr_bf%d" % c, offset=WQR_AT + 2048 if c == 2 else None)
            nc.scalar.copy(out=kr_bf[c][:, u * SUB : (u + 1) * SUB, :], in_=banks[s][:].rearrange("p t j -> p j t"))

        def quantize(name, src, width, tag=None, offset=None):
            codes = sb([P, width], U32, name + "_codes", tag, offset)
            scales = sb([P, width], U8, name + "_plane")
            nc.vector.quantize_mx(out=codes[:].bitcast(FP8X4), scales=scales[:], in_=src.rearrange("p j i -> p (j i)"))
            return codes, scales

        def quantize_keys(c, lo, width, tag=None, offset=None):
            return quantize("kr%d_%d" % (c, lo), kr_bf[c][:, lo : lo + width, :], width, tag, offset) + (c * CHUNK + lo, width)

        def score_product(keys, heads, b):
            codes, scales, j0, width = keys
            bank = new_bank(b, [P, len(heads), width])
            for n, h in enumerate(heads):
                nc.tensor.matmul_mx(
                    out=bank[:, n, :],
                    lhsT=qr[h][0][:].bitcast(FP8X4),
                    lhsT_scale=qr[h][1][:],
                    rhs=codes[:].bitcast(FP8X4),
                    rhs_scale=scales[:],
                    start=True,
                    stop=True,
                )
            return bank, heads, j0, width

        def finish(product, on_scalar):
            bank, heads, j0, width = product
            result = sb([P, len(heads), width], F32, "result%d_%d" % (j0, heads[0]))
            if on_scalar:
                nc.scalar.activation(out=result[:], in_=bank[:], func=ACT.Relu, scale=OUT_SCALE)
            else:
                nc.vector.tensor_scalar(result[:], bank[:], 0.0, OUT_SCALE, ALU.max, ALU.mult)
            nc.sync.dma_start(
                out=out[heads[0] * P : (heads[-1] + 1) * P, j0 : j0 + width].rearrange("(h p) j -> p h j", p=P),
                in_=result[:],
            )

        for c in range(CHUNKS):
            gather(0, c)

        def query_pass(h, a):
            first_stage(q_banks[h], wq, 1, a, x_q[a][0][:, h * P : (h + 1) * P], x_q[a][1][:, h * P : (h + 1) * P])

        def round_queries(h, bank, on_scalar, tag=None):
            qr_bf = sb([P, P, PACK], BF16, "qr_bf%d" % h, tag)
            if on_scalar:
                nc.scalar.copy(out=qr_bf[:], in_=bank[:].rearrange("p t m -> p m t"))
            else:
                nc.vector.tensor_copy(out=qr_bf[:], in_=bank[:].rearrange("p t m -> p m t"))
            return qr_bf

        def both_passes(s, b):
            key_pass(s, 0, b)
            key_pass(s, 1)

        for s in range(8):
            key_pass(s, 0, s)
        for c in range(CHUNKS - 1):
            gather(1, c)
        x_bf = [sb([P, M, PACK], BF16, "x_bf%d" % a, offset=WQR_AT + 1024 if a else None) for a in range(PASSES)]
        for a in range(PASSES):
            nc.gpsimd.tensor_scalar(
                x_bf[a][:],
                x_raw[a][:].rearrange("p i m -> p m i"),
                1.0,
                0.0,
                ALU.mult,
                ALU.add,
            )
        x_q = [quantize("x%d" % a, x_bf[a][:], M) for a in range(PASSES)]
        gather(1, 3, X1_AT)
        wq.append(reorder_words(nc.gpsimd.tensor_copy, "wq1", wq_raw[1][:], WQR_AT + 2048)[:])
        for s in range(8):
            key_pass(s, 1)
            round_keys(s)
        for s in range(8, 11):
            both_passes(s, s - 8)
        q_banks = [new_bank(4 + h, [P, PACK, P]) for h in range(M // P)]
        for a in range(PASSES):
            for h in range(M // P):
                query_pass(h, a)
        keys0 = quantize_keys(0, 0, CHUNK, offset=WQ_AT + 2048)
        qr_bf0 = round_queries(0, q_banks[0], False)
        keys1 = quantize_keys(1, 0, CHUNK, offset=WQ_AT)
        qr = [quantize("qr0", qr_bf0[:], P)]
        qr_bf1 = round_queries(1, q_banks[1], False)
        both_passes(11, 3)
        both_passes(12, 6)
        both_passes(13, 7)
        s00 = score_product(keys0, [0], 4)
        round_keys(8)
        s10 = score_product(keys1, [0], 0)
        finish(s00, False)
        qr.append(quantize("qr1", qr_bf1[:], P))
        round_keys(9)
        both_passes(14, 1)
        s01 = score_product(keys0, [1], 5)
        round_keys(10)
        s11 = score_product(keys1, [1], 2)
        round_keys(11)
        both_passes(15, 3)
        finish(s10, True)
        keys2 = quantize_keys(2, 0, CHUNK, "qr_bf0")
        finish(s01, False)
        round_keys(12)
        finish(s11, True)
        s20 = score_product(keys2, [0], 4)
        s21 = score_product(keys2, [1], 0)
        finish(s20, False)
        round_keys(13)
        keys3a = quantize_keys(3, 0, CHUNK // 2)
        finish(s21, False)
        round_keys(14)
        round_keys(15)
        keys3b = quantize_keys(3, CHUNK // 2, CHUNK // 2)
        s3a = score_product(keys3a, [0, 1], 5)
        s3b0 = score_product(keys3b, [0], 6)
        s3b1 = score_product(keys3b, [1], 7)
        finish(s3a, True)
        finish(s3b0, False)
        finish(s3b1, True)
